import numpy as np, ml_dtypes
CORES = [23,119,17,113]
N = 4
BF = ml_dtypes.bfloat16
def gentries(a):
    return np.ascontiguousarray(a.reshape(8, 16, -1).transpose(0, 2, 1)).reshape(8, -1)
def gtable(e):
    e = np.asarray(e); return np.ascontiguousarray(e.reshape(8, -1, 16).transpose(0, 2, 1)).reshape(128, -1).astype(np.int32)
def f(rng, *shape):
    return (rng.standard_normal(shape, dtype=np.float32) * np.exp2(rng.integers(-2, 3, shape[:-1] + (1,)))).astype(BF)
def wide(rng, *shape):
    v = f(rng, *shape).astype(np.float32); k = shape[:-2] + (1, shape[-1])
    return (v * np.exp2(rng.integers(-6, 7, k)) * (rng.random(k) > 0.0625)).astype(BF)
V, D, C, R = 4096, 2, 64, 2
def ranks(t):
    return t.reshape(8, D, N, V).transpose(2, 0, 1, 3)
def globe(a, bl):
    out = np.zeros((N, 8, D * V), np.int64)
    for r in range(N):
        own = np.broadcast_to(r * V + np.arange(V), (8, V))
        ghosts = (np.arange(N)[:, None, None] * V + bl[:, :, r]).transpose(1, 0, 2).reshape(8, N * C)
        out[r] = np.take_along_axis(np.concatenate([own, ghosts], 1), a[r].reshape(8, D * V).astype(np.int64), 1)
    return out.reshape(N, 8, D, V).transpose(1, 2, 0, 3).reshape(8, D, N * V)
def unpack(nb, bl):
    return np.stack([gentries(t) for t in nb]).reshape(N, 8, D, V), np.stack([gentries(t) for t in bl]).reshape(N, 8, N, C)
def pack(rng, a, bl, v):
    o = np.argsort(rng.random(a.shape), 2); a = np.take_along_axis(a, o, 2); v = np.take_along_axis(v, o, 2)
    return {"nb": np.stack([gtable(t.reshape(8, D * V)) for t in a]), "bl": np.stack([gtable(t.reshape(8, N * C)) for t in bl]),
            "w": np.ascontiguousarray(v).reshape(N, 8, D * V).astype(np.float32).astype(BF), "x": f(rng, N, 128, V)}
def graphs(rng, p):
    bl = np.argsort(rng.random((N, 8, N, V)), axis=-1)[..., :C]
    a = np.full((N, 8, D, V), -1, np.int64)
    for g in range(8):
        for d in range(D):
            for r in range(N):
                for q in range(r):
                    o = rng.permutation(C); u = bl[r, g, q]; t = bl[q, g, r][o]
                    k = (a[r, g, d, u] < 0) & (a[q, g, d, t] < 0) & (rng.random(C) < p)
                    a[r, g, d, u[k]] = V + q * C + o[k]; a[q, g, d, t[k]] = V + r * C + np.flatnonzero(k)
            for r in range(N):
                e = rng.permutation(np.flatnonzero(a[r, g, d] < 0)); h = len(e) // 2
                a[r, g, d, e[:h]] = e[h:2 * h]; a[r, g, d, e[h:2 * h]] = e[:h]
                if len(e) > 2 * h: a[r, g, d, e[-1]] = (e[-1] + 1) % V
        for r in range(N):
            alias = np.full(V, -1, np.int64); alias[bl[r, g, r]] = V + r * C + np.arange(C)
            b = a[r, g]; n = np.where(b < V, alias[np.minimum(b, V - 1)], -1)
            a[r, g] = np.where((n >= 0) & (rng.random((D, V)) < 0.5), n, b)
    return a, bl
def both(a, bl, z):
    return np.array(ranks(np.take_along_axis(z, np.minimum(globe(a, bl), np.arange(N * V)), 2)))
def setup_inputs(rng):
    a, bl = graphs(rng, 0.6)
    return pack(rng, a, bl, both(a, bl, np.exp2(4 * rng.random((8, D, N * V)))))
def setup_inputs_ties(rng):
    a, bl = graphs(rng, 0.6); z = rng.integers(1, 4, (8, D, N * V)).astype(np.float64); z[rng.integers(0, 8)] = 1
    z *= np.exp2(rng.integers(-20, 21, (8, 1, 1)))
    return pack(rng, a, bl, both(a, bl, z))
def setup_inputs_borders(rng):
    a, bl = graphs(rng, 1.0); v = both(a, bl, np.exp2(3 * rng.random((8, D, N * V))))
    far = ranks(globe(a, bl) // V != np.arange(N * V) // V)
    return pack(rng, a, bl, v * np.where(far, 8, 1))
def setup_inputs_hubs(rng):
    a, bl = graphs(rng, 0.6); v = both(a, bl, np.exp2(4 * rng.random((8, D, N * V))))
    for r in range(N):
        for g in range(8):
            e = rng.permutation(V); h = e[:16]; leaves = e[16:V // 2]; b = a[r, g]; c = v[r, g]
            b[:, leaves] = h[rng.integers(0, 16, (D, len(leaves)))]
            b[0, h] = h[np.arange(16) ^ 1]; c[0, h] = 256
    return pack(rng, a, bl, v)
def setup_inputs_any(rng):
    bl = rng.integers(0, V, (N, 8, N, C)); bl[..., C // 2:] = bl[..., :1]; bl[..., 1] = 0; bl[..., 2] = V - 1
    a = rng.integers(0, V + N * C, (N, 8, D, V)); j = np.arange(V)
    a = np.where(ranks(globe(a, bl) == np.arange(N * V)), (j + 1) % V, a)
    o = rng.permutation(8); a[:, o[0]] = (j + 1) % V; a[:, o[1]] = j ^ 1
    for r in range(N):
        for g in o[2:5]:
            q = r ^ 1
            a[r, g, :, bl[r, g, q, 0]] = V + q * C + rng.choice(np.r_[0, C // 2:C], D)
    return pack(rng, a, bl, np.exp2(4 * rng.random((N, 8, D, V))))
def setup_inputs_spread(rng):
    a, bl = graphs(rng, 0.6); z = np.exp2(rng.integers(-3, 4, (8, D, N * V)) + rng.random((8, D, N * V)))
    d = pack(rng, a, bl, both(a, bl, z)); d["x"] = wide(rng, N, 128, V); return d
def check_inputs(d):
    bad = []
    if d["bl"].min() < 0 or d["bl"].max() >= V: bad.append("bl")
    if d["nb"].min() < 0 or d["nb"].max() >= V + N * C: bad.append("nb")
    if not bad and (globe(*unpack(d["nb"], d["bl"])) == np.arange(N * V)).any(): bad.append("own neighbour")
    u = d["w"].astype(np.float32)
    if not (np.isfinite(u).all() and (u > 0).all()): bad.append("w")
    v = np.abs(d["x"].astype(np.float32))
    if not np.isfinite(v).all(): bad.append("x")
    if not 4.0 * D * float(u.max()) * float(v.max()) < 2.0 ** 127: bad.append("range")
    return bad
def reference(nb, bl, w, x):
    i = np.arange(N * V); A = globe(*unpack(nb, bl))
    u = w.astype(np.float64).reshape(N, 8, D, V).transpose(1, 2, 0, 3).reshape(8, D, N * V)
    mate = np.tile(i, (8, 1)); free = np.ones((8, N * V), bool)
    for t in range(R):
        k = np.where(np.take_along_axis(free[:, None], A, 2), u, 0.0)
        P = np.take_along_axis(A, np.argmax(k, 1)[:, None], 1)[:, 0]
        P = np.where(free & (np.max(k, 1) > 0), P, -1)
        hit = (P >= 0) & (np.take_along_axis(P, np.maximum(P, 0), 1) == i)
        mate = np.where(hit, P, mate); free = free & ~hit
    two = mate != i; first = np.minimum(mate, i); rep = first == i
    num = (np.add.accumulate(rep.reshape(8, N, V).astype(np.int64), 2) - 1 + V * np.arange(N)[:, None]).reshape(8, N * V)
    cm = np.take_along_axis(num, first, 1).reshape(8, N, V)
    xx = np.ascontiguousarray(x.astype(np.float64).reshape(N, 8, 16, V).transpose(1, 2, 0, 3)).reshape(8, 16, N * V)
    X = xx + np.where(two[:, None], np.take_along_axis(xx, mate[:, None], 2), 0.0)
    s = np.zeros((8, 16, N * V))
    for d in range(D):
        s += u[:, d, None] * np.take_along_axis(X, A[:, d, None], 2)
    s = s + np.where(two[:, None], np.take_along_axis(s, mate[:, None], 2), 0.0)
    y = np.zeros((8, 16, N * V))
    for g in range(8):
        y[g][:, num[g, rep[g]]] = s[g][:, rep[g]]
    y = np.ascontiguousarray(y.reshape(8, 16, N, V).transpose(2, 0, 1, 3)).reshape(N, 128, V)
    return {"y": y.astype(np.float32), "cm": np.stack([gtable(cm[:, r]) for r in range(N)]).astype(np.float32)}

@@ -1,0 +1,366 @@
+import numpy as np
+from concourse.bass import DstId, RemoteDMATransfer
+from concourse.mybir import AluOpType, ActivationFunctionType
+
+V, C, N = 4096, 64, 4
+GH = V + N * C
+ZC = GH
+CH = 512
+DUMP = 512
+
+SCRATCH = {}
+
+
+def _declare(names, cols, dtype, rows=128):
+    for n in names.split():
+        SCRATCH[n] = ("sbuf", [rows, cols] if isinstance(cols, int) else [rows] + list(cols), dtype)
+
+
+_declare("bli blg ioh ioa", 16, "int32")
+_declare("blu blgu", 16, "uint16")
+_declare("nbi", 512, "int32")
+_declare("nbu", 512, "uint16")
+_declare("z", (2, 16, 16), "bfloat16")
+_declare("wb", 512, "bfloat16")
+_declare("u1 uo u2 mo pos cl", 256, "uint16")
+_declare("u1f uof u2f dif tmp tm2 mof num inc cms ivb idm vb dm dmo fd zz mant s4 s5 s6", 256, "float32")
+_declare("pf p1b p2b m1 m2 lt1 lt2 nr1 nr2 nr rep z1 t2 cq bq eb s1 s2 s3 sx", 256, "bfloat16")
+_declare("im", 256, "int32")
+_declare("itri", 128, "int32")
+_declare("ohf", 16, "float32")
+_declare("ohb", 16, "bfloat16")
+_declare("igh iga", 8, "int32")
+_declare("ghb", 8, "bfloat16")
+_declare("icc", 2, "int32")
+_declare("gcol", 2, "float32")
+_declare("ir8 ira", 128, "int32", 8)
+_declare("r8", 128, "bfloat16", 8)
+_declare("osel", 2048, "bfloat16")
+_declare("oself", 2048, "float32")
+_declare("bo ntt nt idn", 128, "bfloat16")
+_declare("we wp1 wm wp2", GH, "bfloat16")
+_declare("wn fx", GH, "float32")
+_declare("gat", 2 * V, "bfloat16")
+_declare("gatn g1", V, "float32")
+_declare("xc wr0", V, "bfloat16")
+_declare("xw", GH + 16, "bfloat16")
+_declare("sw", GH + 16, "float32")
+_declare("w8", V, "bfloat16", 8)
+_declare("yb", DUMP + V, "float32")
+for _i in range(8):
+    SCRATCH["ps%d" % _i] = ("psum", [128, 512], "float32")
+
+EXCH = ["x0", "x1", "x2", "xx", "x3", "x4", "x6", "x5"]
+LOADS = ["lbl", "lnb", "lw", "lx", "lwr", "lw8", "sty", "stc"]
+SEMAPHORES = ["v", "a", "t", "q", "sent"] + EXCH + LOADS
+
+
+def link_engines(topo, cores, src):
+    on = [d for d in cores if d != src and topo.chip(d) == topo.chip(src)]
+    off = [d for d in cores if d != src and topo.chip(d) != topo.chip(src)]
+    out, used = {}, []
+    for d in off + on:
+        left = [e for e in topo.engines(src, d) if e not in used]
+        if d in on and off:
+            far = topo.engines(src, off[0])
+            left = [e for e in left if e not in far] or left
+        out[d] = left[:4]
+        used += out[d]
+    return out
+
+
+def rank_program(g, core, T, topo):
+    r = T.rank_of(core)
+    if r is None:
+        return
+    A = AluOpType
+    COPY = ActivationFunctionType.Copy
+    cores = list(T.cores)
+    Q = {"v": g.vector, "a": g.scalar, "t": g.tensor, "g": g, "y": g.sync}
+    SEM = {"v": "v", "a": "a", "t": "t", "g": "q"}
+    cnt = {s: 0 for s in SEMAPHORES}
+    seen = {}
+
+    def wait(qn, deps):
+        best = {}
+        for d in deps:
+            if d is not None:
+                best[d[0]] = max(best.get(d[0], 0), d[1])
+        for s, n in best.items():
+            if seen.get((qn, s), 0) < n:
+                Q[qn].wait_ge(T.sem[s], n)
+                seen[(qn, s)] = n
+
+    def op(qn, fn, *args, deps=(), **kw):
+        wait(qn, deps)
+        fn(*args, **kw).then_inc(T.sem[SEM[qn]], 1)
+        cnt[SEM[qn]] += 1
+        return (SEM[qn], cnt[SEM[qn]])
+
+    def dma(qn, sem, out, in_, deps=()):
+        wait(qn, deps)
+        Q[qn].dma_start(out, in_).then_inc(T.sem[sem], 16)
+        cnt[sem] += 16
+        return (sem, cnt[sem])
+
+    def tt(o, a, b, f, *deps):
+        return op("v", g.vector.tensor_tensor, o, a, b, f, deps=deps)
+
+    def ts(o, a, s1, f, *deps):
+        return op("v", g.vector.tensor_scalar, o, a, s1, None, f, deps=deps)
+
+    def cp(o, a, *deps):
+        return op("v", g.vector.tensor_copy, o, a, deps=deps)
+
+    def acp(o, a, *deps, **kw):
+        return op("a", g.scalar.activation, o, a, COPY, deps=deps, **kw)
+
+    mine = link_engines(topo, cores, core)
+
+    def exchange(sem, src, piece, dst, place, *deps):
+        wait("g", deps)
+        tr = []
+        for q in range(N):
+            if q == r:
+                continue
+            d = cores[q]
+            a = topo.addr(d)
+            a0, a1 = piece(q)
+            tr.append(RemoteDMATransfer(dst_ids=[DstId(rid=a[0], pnc=a[1])],
+                                        dma_engine_mask=sum(1 << e for e in mine[d]), remote_sem=T.sem[sem],
+                                        srcs=[src[:, a0:a1]], dsts=[dst[:, place[0]:place[1]]]))
+        g.remote_dma_fused(tr, local_sem=T.sem.sent)
+        cnt["sent"] += sum(len(mine[d]) for d in mine)
+        cnt[sem] += sum(len(link_engines(topo, cores, c)[core]) for c in cores if c != core)
+        return (sem, cnt[sem])
+
+    def slots(q):
+        return (C * q, C * q + C)
+
+    own = slots(r)
+    GO = (V + C * r, V + C * r + C)
+
+    def border(eng, buf, snd, *deps):
+        src = buf[:, 0:V].indirect(T.blu[:])
+        return cp(snd[:], src, *deps) if eng == "v" else acp(snd[:], src, *deps)
+
+    k_bl = dma("y", "lbl", T.bli[:], T.bl[:])
+    k_nb = dma("y", "lnb", T.nbi[:], T.nb[:])
+    dma("a", "lw", T.z[:, 0], T.w[0::2, :])
+    k_w = dma("a", "lw", T.z[:, 1], T.w[1::2, :])
+
+    q_gh = op("g", g.iota, T.igh[:], [[-16, 8]], 0, 1)
+    q_oh = op("g", g.iota, T.ioh[:], [[-1, 16]], 16, 1)
+    q_im = op("g", g.iota, T.im[:], [[0, 32], [16, 8]], 128, 1)
+    a_x0 = exchange("x0", T.bli, lambda q: (4 * q, 4 * q + 4), T.blg, (4 * r, 4 * r + 4), k_bl)
+    q_r8 = op("g", g.iota, T.ir8[:], [[1, 128]], 0, -16)
+    q_tri = op("g", g.iota, T.itri[:], [[1, 128]], 0, -1)
+    q_vb = op("g", g.iota, T.ivb[:], [[16, 256]], 0, 1, allow_small_or_imprecise_dtypes=True)
+    q_dm = op("g", g.iota, T.idm[:], [[0, 8], [16, 32]], 0, 1, allow_small_or_imprecise_dtypes=True)
+
+    v0 = op("v", g.vector.memset, T.zz[:], 0.0)
+    v1 = op("v", g.vector.memset, T.fd[:], 1.0)
+    c1 = ts(T.iga[:], T.igh[:], 4, A.arith_shift_right, q_gh)
+    v2 = op("v", g.vector.memset, T.fd[:, 8:256:8], 2.0, deps=[v1])
+    c4 = ts(T.ghb[:], T.iga[:], 0, A.is_equal, c1)
+    c2 = ts(T.icc[:, 0:1], T.igh[:, 0:1], 15, A.bitwise_and, q_gh)
+    c3 = ts(T.ioa[:], T.ioh[:], 15, A.bitwise_and, q_oh)
+    fe = op("v", g.vector.tensor_tensor_scan, T.ps7[:, 0:256], T.fd[:], T.zz[:], float(2.0 ** (32 * r - 71)), A.mult, A.add, deps=[v2, v0])
+    c5 = tt(T.gcol[:, 0:1], T.icc[:, 0:1], T.igh[:, 0:1], A.subtract, c2)
+    c6 = ts(T.ohf[:], T.ioa[:], 0, A.is_equal, c3)
+    c7 = ts(T.ohb[:], T.ioa[:], 0, A.is_equal, c3)
+    mt = ts(T.mant[:], T.im[:], T.gcol[:, 0:1], A.add, q_im, c5)
+    eb = tt(T.eb[:], T.mant[:], T.ps7[:, 0:256], A.mult, mt, fe)
+
+    for c in range(8):
+        a0 = acp(T.osel[:, 256 * c:256 * c + 256], T.zz[:], v0)
+    for c in range(16):
+        k_os = acp(T.osel[:, 129 * c:128 * (c + 1):16], T.ghb[:], c4, a0)
+
+    def build(win, src, c_src, nv=11):
+        tv = ta = None
+        for c in range(16):
+            if c < nv:
+                tv = ts(win[:, c:V:16], src[:], T.ohb[:, c:c + 1], A.mult, c_src, c7)
+            else:
+                ta = acp(win[:, c:V:16], src[:], c_src, c6, scale=T.ohf[:, c:c + 1])
+        return [x for x in (tv, ta) if x is not None]
+
+    k_we = build(T.we, T.eb, eb)
+    for c in range(16):
+        k_bo = acp(T.bo[:, c:128:16], T.ghb[:])
+
+    for b in range(16):
+        k_wb = op("v", g.vector.transpose, T.wb[:, b:512:16], T.z[:, :, b, :], deps=[k_w])
+    b1 = cp(T.blu[:], T.bli[:], k_bl)
+    b2 = cp(T.blg[:, 4 * r:4 * r + 4], T.bli[:, 4 * r:4 * r + 4], k_bl)
+    d1 = tt(T.ps5[:, 0:256], T.nbi[:, 0:256], T.nbi[:, 256:512], A.subtract, k_nb)
+    d2 = tt(T.pf[:], T.wb[:, 0:256], T.wb[:, 256:512], A.is_ge, k_wb)
+    d3 = tt(T.ps5[:, 256:512], T.pf[:], T.ps5[:, 0:256], A.mult, d2, d1)
+    d4 = tt(T.u1f[:], T.nbi[:, 256:512], T.ps5[:, 256:512], A.add, d3)
+    k_u1 = cp(T.u1[:], T.u1f[:], d4)
+    b3 = cp(T.blgu[:], T.blg[:], a_x0, b2)
+    for q in range(N):
+        k_we2 = op("v", g.vector.tensor_scalar, T.we[:, V + C * q:V + C * q + C],
+                   T.we[:, 0:V].indirect(T.blgu[:, 4 * q:4 * q + 4]), float(2.0 ** (32 * (q - r))), None, A.mult,
+                   deps=[b3] + k_we)
+
+    dma("y", "lx", T.xw[:, 0:V], T.x[:], [a_x0])
+    k_x = dma("y", "lx", T.xc[:], T.x[:])
+
+    PARTS = [("v", 0, 64), ("a", 128, 64), ("v", 64, 64), ("a", 192, 64)]
+
+    def lookup(win, lst, deps, ps, gat, g0, sel, parts=PARTS, psdeps=()):
+        tok = None
+        for e, k0, nk in parts:
+            out = gat[:, g0 + 16 * k0:g0 + 16 * (k0 + nk)]
+            src = win[:].indirect(lst[:, k0:k0 + nk])
+            x = cp(out, src, *deps) if e == "v" else acp(out, src, *deps)
+            wait("t", [x, k_os] + list(psdeps))
+            for c in range(16):
+                args = (ps[:, k0:k0 + nk], sel[:, 128 * c:128 * c + 128], gat[:, g0 + 16 * k0 + c:g0 + 16 * (k0 + nk):16], c == 0, c == 15)
+                if c < 15:
+                    g.tensor.matmul(*args)
+                else:
+                    tok = op("t", g.tensor.matmul, *args)
+        return tok
+
+    k_p1 = lookup(T.we, T.u1, k_we + [k_we2, k_u1], T.ps0, T.gat, 0, T.osel)
+    p1 = cp(T.p1b[:], T.ps0[:, 0:256], k_p1)
+    k_w1 = build(T.wp1, T.p1b, p1)
+    o1 = border("v", T.wp1, T.s1, b1, *k_w1)
+    a_x1 = exchange("x1", T.s1, slots, T.wp1, GO, o1)
+    z_1 = acp(T.wp1[:, GO[0]:GO[1]], T.s1[:, own[0]:own[1]], o1)
+    e1 = tt(T.uof[:], T.nbi[:, 0:256], T.ps5[:, 256:512], A.subtract, d3)
+    k_uo = cp(T.uo[:], T.uof[:], e1)
+    k_po = lookup(T.we, T.uo, k_we + [k_we2, k_uo], T.ps1, T.gat, 4096, T.osel)
+    k_lt1 = tt(T.lt1[:], T.p1b[:], T.eb[:], A.is_lt)
+    k_um = ts(T.tmp[:], T.u1f[:], float(-ZC), A.add, d4)
+    vx = op("v", g.vector.memset, T.xw[:, ZC:ZC + 16], 0.0)
+    vs = op("v", g.vector.memset, T.sw[:, ZC:ZC + 16], 0.0)
+
+    k_r1 = lookup(T.wp1, T.u1, k_w1 + [a_x1, z_1], T.ps2, T.gat, 0, T.osel)
+    m1 = tt(T.m1[:], T.ps2[:, 0:256], T.eb[:], A.is_equal, k_r1)
+    k_wm = build(T.wm, T.m1, m1)
+    o2 = border("v", T.wm, T.s2, *k_wm)
+    a_x2 = exchange("x2", T.s2, slots, T.wm, GO, o2)
+    z_2 = acp(T.wm[:, GO[0]:GO[1]], T.s2[:, own[0]:own[1]], o2)
+    for c in range(16):
+        k_wr = dma("y", "lwr", T.wr0[c:128:16, :], T.w[:, 0:V], [a_x1])
+    k_w8 = dma("y", "lw8", T.w8[:], T.w[:, V:2 * V])
+    ox = border("v", T.xw, T.sx, k_x)
+    a_xx = exchange("xx", T.sx, slots, T.xw, GO, ox)
+    z_x = acp(T.xw[:, GO[0]:GO[1]], T.sx[:, own[0]:own[1]], ox)
+    q_y1 = op("g", g.iota, T.yb[:, DUMP:DUMP + V // 2], [[0, V // 2]], 0, 0, allow_small_or_imprecise_dtypes=True)
+    k_nr1 = tt(T.nr1[:], T.m1[:], T.lt1[:], A.mult, k_lt1)
+    f1 = tt(T.tm2[:], T.m1[:], T.tmp[:], A.mult, k_um)
+    k_d = tt(T.dif[:], T.u1f[:], T.uof[:], A.subtract, e1)
+
+    k_a1 = lookup(T.wm, T.u1, k_wm + [a_x2, z_2], T.ps3, T.gat, 0, T.osel)
+    k_ao = lookup(T.wm, T.uo, k_wm + [a_x2, z_2], T.ps4, T.gat, 4096, T.osel)
+    h1 = ts(T.z1[:], T.ps3[:, 0:256], 0.0, A.is_equal, k_a1)
+    h2 = tt(T.ps5[:, 0:256], T.z1[:], T.ps0[:, 0:256], A.mult, h1)
+    h3 = tt(T.ps5[:, 256:512], T.m1[:], T.ps4[:, 0:256], A.add, k_ao)
+    h4 = tt(T.t2[:], T.z1[:], T.ps5[:, 256:512], A.add, h3)
+    h5 = ts(T.cq[:], T.t2[:], 0.0, A.is_equal, h4)
+    h6 = tt(T.bq[:], T.cq[:], T.ps1[:, 0:256], A.mult, h5, k_po)
+    p2 = tt(T.p2b[:], T.bq[:], T.ps5[:, 0:256], A.add, h6, h2)
+    k_w2 = build(T.wp2, T.p2b, p2)
+    o3 = border("v", T.wp2, T.s3, *k_w2)
+    a_x3 = exchange("x3", T.s3, slots, T.wp2, GO, o3)
+    z_3 = acp(T.wp2[:, GO[0]:GO[1]], T.s3[:, own[0]:own[1]], o3)
+    q_y2 = op("g", g.iota, T.yb[:, DUMP + V // 2:DUMP + V], [[0, V // 2]], 0, 0, allow_small_or_imprecise_dtypes=True)
+    i1 = tt(T.tmp[:], T.z1[:], T.dif[:], A.mult, k_d, f1)
+    k_A = ts(T.ps5[:, 256:512], T.tm2[:], float(ZC), A.add, f1)
+    i2 = tt(T.u2f[:], T.uof[:], T.tmp[:], A.add, i1)
+    k_lt2 = tt(T.lt2[:], T.p2b[:], T.eb[:], A.is_lt, p2)
+    k_u2 = cp(T.u2[:], T.u2f[:], i2)
+    k_B = ts(T.ps5[:, 0:256], T.u2f[:], float(-ZC), A.add, i2, p2)
+    k_nbu = cp(T.nbu[:], T.nbi[:])
+    n1 = op("v", g.vector.tensor_scalar, T.ntt[:], T.itri[:], 0, -1.0, A.is_le, A.mult, deps=[q_tri])
+    n3 = ts(T.ira[:], T.ir8[:], 4, A.arith_shift_right, q_r8)
+    n5 = ts(T.vb[:], T.ivb[:], T.gcol[:, 0:1], A.add, q_vb)
+    n6 = ts(T.dm[:], T.idm[:], T.gcol[:, 0:1], A.add, q_dm)
+    n2 = tt(T.nt[:], T.ntt[:], T.bo[:], A.mult, n1, k_bo)
+    n4 = ts(T.r8[:], T.ira[:], 0, A.is_equal, n3)
+    n7 = ts(T.dmo[:], T.dm[:], float(4096 * r - DUMP), A.add, n6)
+    n8 = ts(T.idn[:], T.itri[:], 0, A.is_equal)
+    k_of = acp(T.oself[:], T.osel[:])
+
+    k_r2 = lookup(T.wp2, T.u2, k_w2 + [a_x3, z_3, k_u2], T.ps2, T.gat, 0, T.osel)
+    m2 = tt(T.m2[:], T.ps2[:, 0:256], T.eb[:], A.is_equal, k_r2)
+    j1 = tt(T.tmp[:], T.m2[:], T.ps5[:, 0:256], A.mult, m2, k_B)
+    j2 = tt(T.mof[:], T.tmp[:], T.ps5[:, 256:512], A.add, j1, k_A)
+    k_mo = cp(T.mo[:], T.mof[:], j2)
+
+    NC = V // CH
+    KC = CH // 16
+    FD = 5 * CH
+    dep_x = [k_mo, k_x, a_xx, z_x, vx]
+    k_fv = tt(T.fx[:, 0:FD], T.xw[:].indirect(T.mo[:, 0:FD // 16]), T.xc[:, 0:FD], A.add, *dep_x)
+    banks = [T.ps0, T.ps1, T.ps3]
+    gx, px = [], []
+    for j in range(3):
+        sl = slice(FD + CH * j, FD + CH * (j + 1))
+        gx.append(acp(T.gat[:, sl], T.xw[:].indirect(T.mo[:, (FD + CH * j) // 16:(FD + CH * (j + 1)) // 16]), *dep_x))
+        wait("t", [n8, k_x, p2])
+        g.tensor.matmul(banks[j][:], T.idn[:], T.xc[:, sl], True, False)
+        px.append(op("t", g.tensor.matmul, banks[j][:], T.idn[:], T.gat[:, sl], False, True, deps=[gx[j]]))
+        if j >= 1:
+            k_fa = acp(T.fx[:, FD + CH * (j - 1):FD + CH * j], banks[j - 1][:], px[j - 1])
+    k_fa = acp(T.fx[:, FD + 2 * CH:V], banks[2][:], px[2])
+    o4 = border("v", T.fx, T.s4, k_fv, k_fa)
+    a_x4 = exchange("x4", T.s4, slots, T.fx, GO, o4)
+    z_4 = acp(T.fx[:, GO[0]:GO[1]], T.s4[:, own[0]:own[1]], o4)
+
+    r1 = tt(T.nr2[:], T.m2[:], T.lt2[:], A.mult, k_lt2)
+    r2 = tt(T.nr[:], T.nr2[:], T.nr1[:], A.add, r1, k_nr1)
+    k_rep = ts(T.rep[:], T.nr[:], 0.0, A.is_equal, r2)
+    op("t", g.tensor.matmul, T.ps6[:, 0:256], T.bo[:], T.rep[:], True, True, deps=[k_rep, k_bo])
+    k_pn = op("t", g.tensor.matmul, T.ps6[:, 256:512], T.nt[:], T.rep[:], True, True, deps=[n2])
+    l1 = tt(T.tmp[:], T.mof[:], T.vb[:], A.subtract, n5)
+    k_in = op("v", g.vector.tensor_tensor_scan, T.inc[:], T.ps6[:, 0:256], T.zz[:], float(4096 * r), A.add, A.add, deps=[k_pn])
+    l2 = tt(T.tm2[:], T.nr[:], T.tmp[:], A.mult, l1, k_A)
+    k_num = tt(T.num[:], T.inc[:], T.ps6[:, 256:512], A.add, k_in)
+    l3 = tt(T.dif[:], T.tm2[:], T.vb[:], A.add, l2)
+    l4 = tt(T.uof[:], T.num[:], T.dmo[:], A.subtract, k_num, n7)
+    k_cl = cp(T.cl[:], T.dif[:], l3)
+    l5 = tt(T.mant[:], T.uof[:], T.rep[:], A.mult, l4)
+    l6 = tt(T.inc[:], T.mant[:], T.dm[:], A.add, l5, k_num)
+    k_pos = cp(T.pos[:], T.inc[:], l6)
+
+    dep_f = [k_fv, k_fa, a_x4, z_4]
+    t0, mm, ss, gg, pw = {}, {}, {}, {}, {}
+    for i in range(NC + 2):
+        if i < NC:
+            sl = slice(CH * i, CH * i + CH)
+            gg[i] = acp(T.g1[:, sl], T.fx[:].indirect(T.nbu[:, 256 + KC * i:256 + KC * (i + 1)]), k_nbu, *dep_f)
+            pw[i] = op("t", g.tensor.matmul, T["ps%d" % (i % 2)][:], T.r8[:], T.w8[:, sl], True, True, deps=[n4, k_w8, k_fa, mm.get(i - 2)])
+            t0[i] = tt(T.sw[:, sl], T.fx[:].indirect(T.nbu[:, KC * i:KC * (i + 1)]), T.wr0[:, sl], A.mult, k_wr, *dep_f)
+        if 0 <= i - 1 < NC:
+            k = i - 1
+            sl = slice(CH * k, CH * k + CH)
+            mm[k] = tt(T["ps%d" % (2 + k % 3)][:], T.g1[:, sl], T["ps%d" % (k % 2)][:], A.mult, gg[k], pw[k], ss.get(k - 3))
+        if 0 <= i - 2 < NC:
+            k = i - 2
+            sl = slice(CH * k, CH * k + CH)
+            ss[k] = tt(T.sw[:, sl], T.sw[:, sl], T["ps%d" % (2 + k % 3)][:], A.add, t0[k], mm[k])
+
+    k_wn = build(T.wn, T.num, k_num, nv=0)
+    o6 = border("a", T.wn, T.s6, *k_wn)
+    a_x6 = exchange("x6", T.s6, slots, T.wn, GO, o6)
+    z_6 = acp(T.wn[:, GO[0]:GO[1]], T.s6[:, own[0]:own[1]], o6)
+    o5 = border("v", T.sw, T.s5, ss[NC - 1])
+    a_x5 = exchange("x5", T.s5, slots, T.sw, GO, o5)
+    z_5 = acp(T.sw[:, GO[0]:GO[1]], T.s5[:, own[0]:own[1]], o5)
+    k_cm = lookup(T.wn, T.cl, k_wn + [a_x6, z_6, k_cl], T.ps7, T.gatn, 0, T.oself, psdeps=[k_of])
+
+    w = None
+    for i in range(NC - 1, -1, -1):
+        sl = slice(CH * i, CH * i + CH)
+        x = acp(T.g1[:, sl], T.sw[:].indirect(T.mo[:, KC * i:KC * (i + 1)]), a_x5, z_5, vs, mm[NC - 1], k_mo, ss[NC - 1])
+        w = tt(T.yb[:, 0:DUMP + CH * (i + 1)].indirect(T.pos[:, KC * i:KC * (i + 1)]), T.sw[:, sl], T.g1[:, sl], A.add, x, w, k_pos, q_y1, q_y2)
+        k_y = dma("y", "sty", T.y[:, sl], T.yb[:, DUMP + CH * i:DUMP + CH * (i + 1)], [w])
+    k_c = acp(T.cms[:], T.ps7[:, 0:256], k_cm)
+    k_st = dma("y", "stc", T.cm[:], T.cms[:], [k_c])
+    wait("y", [(s, cnt[s]) for s in SEMAPHORES if cnt[s]])

@@ -16,29 +16,28 @@ def _declare(names, cols, dtype, rows=128):
         SCRATCH[n] = ("sbuf", [rows, cols] if isinstance(cols, int) else [rows] + list(cols), dtype)
 
 
-_declare("bli blg ioh ioa", 16, "int32")
-_declare("blu blgu", 16, "uint16")
+_declare("bli blg ioh ioa bla blb", 16, "int32")
+_declare("blu blgu blh bl15", 16, "uint16")
+_declare("nbb", 32, "uint16")
 _declare("nbi", 512, "int32")
 _declare("nbu", 512, "uint16")
 _declare("z", (2, 16, 16), "bfloat16")
-_declare("wb", 512, "bfloat16")
+_declare("wb wbs", 512, "bfloat16")
 _declare("u1 uo u2 mo pos cl", 256, "uint16")
-_declare("u1f uof u2f dif tmp tm2 mof num inc cms ivb idm vb dm dmo fd zz mant s4 s5 s6", 256, "float32")
-_declare("pf p1b p2b m1 m2 lt1 lt2 nr1 nr2 nr rep z1 t2 cq bq eb s1 s2 s3 sx", 256, "bfloat16")
+_declare("u1f uof u2f dif tmp tm2 mof num inc cms ivb idm dm dmo fd zz mant s4 s5 s6 nbm0 nbm1 tb0 tb1", 256, "float32")
+_declare("pf p1b p2b m1 m2 nr1 nr rep z1 t2 cq bq eb s1 s2 s3 sx blm wbm0 wbm1", 256, "bfloat16")
 _declare("im", 256, "int32")
-_declare("itri", 128, "int32")
 _declare("ohf", 16, "float32")
 _declare("ohb", 16, "bfloat16")
 _declare("igh iga", 8, "int32")
 _declare("ghb", 8, "bfloat16")
 _declare("icc", 2, "int32")
-_declare("gcol", 2, "float32")
-_declare("ir8 ira", 128, "int32", 8)
+_declare("gcol gco2", 2, "float32")
 _declare("r8", 128, "bfloat16", 8)
 _declare("osel", 2048, "bfloat16")
 _declare("oself", 2048, "float32")
-_declare("bo ntt nt idn", 128, "bfloat16")
-_declare("we wp1 wm wp2", GH, "bfloat16")
+_declare("bo nt idn", 128, "bfloat16")
+_declare("we wp wm", GH, "bfloat16")
 _declare("wn fx", GH, "float32")
 _declare("gat", 2 * V, "bfloat16")
 _declare("gatn g1", V, "float32")
@@ -51,7 +50,7 @@ for _i in range(8):
     SCRATCH["ps%d" % _i] = ("psum", [128, 512], "float32")
 
 EXCH = ["x0", "x1", "x2", "xx", "x3", "x4", "x6", "x5"]
-LOADS = ["lbl", "lnb", "lw", "lx", "lwr", "lw8", "sty", "stc"]
+LOADS = ["lbl", "lnb", "lw", "lx", "lwr", "lw8", "lr8", "sty", "stc"]
 SEMAPHORES = ["v", "a", "t", "q", "sent"] + EXCH + LOADS
 
 
@@ -75,6 +74,7 @@ def rank_program(g, core, T, topo):
         return
     A = AluOpType
     COPY = ActivationFunctionType.Copy
+    IDENT = ActivationFunctionType.Identity
     cores = list(T.cores)
     Q = {"v": g.vector, "a": g.scalar, "t": g.tensor, "g": g, "y": g.sync}
     SEM = {"v": "v", "a": "a", "t": "t", "g": "q"}
@@ -115,6 +115,9 @@ def rank_program(g, core, T, topo):
     def acp(o, a, *deps, **kw):
         return op("a", g.scalar.activation, o, a, COPY, deps=deps, **kw)
 
+    def plus(o, a, b, *deps):
+        return op("a", g.scalar.activation, o, a, IDENT, bias=b, deps=deps)
+
     mine = link_engines(topo, cores, core)
 
     def exchange(sem, src, piece, dst, place, *deps):
@@ -140,9 +143,8 @@ def rank_program(g, core, T, topo):
     own = slots(r)
     GO = (V + C * r, V + C * r + C)
 
-    def border(eng, buf, snd, *deps):
-        src = buf[:, 0:V].indirect(T.blu[:])
-        return cp(snd[:], src, *deps) if eng == "v" else acp(snd[:], src, *deps)
+    def border(buf, snd, *deps):
+        return cp(snd[:], buf[:, 0:V].indirect(T.blu[:]), *deps)
 
     k_bl = dma("y", "lbl", T.bli[:], T.bl[:])
     k_nb = dma("y", "lnb", T.nbi[:], T.nb[:])
@@ -153,10 +155,13 @@ def rank_program(g, core, T, topo):
     q_oh = op("g", g.iota, T.ioh[:], [[-1, 16]], 16, 1)
     q_im = op("g", g.iota, T.im[:], [[0, 32], [16, 8]], 128, 1)
     a_x0 = exchange("x0", T.bli, lambda q: (4 * q, 4 * q + 4), T.blg, (4 * r, 4 * r + 4), k_bl)
-    q_r8 = op("g", g.iota, T.ir8[:], [[1, 128]], 0, -16)
-    q_tri = op("g", g.iota, T.itri[:], [[1, 128]], 0, -1)
+    q1 = op("g", g.iota, T.bo[:], [[0, 128]], 1, 0, allow_small_or_imprecise_dtypes=True)
+    q2 = op("g", g.affine_select, T.bo[:], T.bo[:], [[-16, 8], [0, 16]], A.is_ge, 0.0, 0, 1, deps=[q1])
+    q_bo = op("g", g.affine_select, T.bo[:], T.bo[:], [[16, 8], [0, 16]], A.is_ge, 0.0, 15, -1, deps=[q2])
     q_vb = op("g", g.iota, T.ivb[:], [[16, 256]], 0, 1, allow_small_or_imprecise_dtypes=True)
     q_dm = op("g", g.iota, T.idm[:], [[0, 8], [16, 32]], 0, 1, allow_small_or_imprecise_dtypes=True)
+    q_nt = op("g", g.affine_select, T.nt[:], T.bo[:], [[-1, 128]], A.is_ge, 0.0, 0, 1, deps=[q_bo])
+    q_id = op("g", g.affine_select, T.idn[:], T.bo[:], [[-1, 128]], A.is_equal, 0.0, 0, 1, deps=[q_bo])
 
     v0 = op("v", g.vector.memset, T.zz[:], 0.0)
     v1 = op("v", g.vector.memset, T.fd[:], 1.0)
@@ -177,24 +182,26 @@ def rank_program(g, core, T, topo):
     for c in range(16):
         k_os = acp(T.osel[:, 129 * c:128 * (c + 1):16], T.ghb[:], c4, a0)
 
-    def build(win, src, c_src, nv=11):
+    def build(win, src, c_src, nv=10, blocks=range(16)):
         tv = ta = None
-        for c in range(16):
+        for c in blocks:
             if c < nv:
                 tv = ts(win[:, c:V:16], src[:], T.ohb[:, c:c + 1], A.mult, c_src, c7)
             else:
                 ta = acp(win[:, c:V:16], src[:], c_src, c6, scale=T.ohf[:, c:c + 1])
         return [x for x in (tv, ta) if x is not None]
 
-    k_we = build(T.we, T.eb, eb)
-    for c in range(16):
-        k_bo = acp(T.bo[:, c:128:16], T.ghb[:])
+    k_we = build(T.we, T.eb, eb, nv=6)
 
+    d1 = tt(T.ps5[:, 0:256], T.nbi[:, 0:256], T.nbi[:, 256:512], A.subtract, k_nb)
+    b1 = cp(T.blu[:], T.bli[:], k_bl)
+    b2 = cp(T.blg[:, 4 * r:4 * r + 4], T.bli[:, 4 * r:4 * r + 4])
+    b4 = ts(T.bla[:], T.bli[:], 4, A.arith_shift_right)
+    b5 = ts(T.blb[:], T.bli[:], 15, A.bitwise_and)
     for b in range(16):
         k_wb = op("v", g.vector.transpose, T.wb[:, b:512:16], T.z[:, :, b, :], deps=[k_w])
-    b1 = cp(T.blu[:], T.bli[:], k_bl)
-    b2 = cp(T.blg[:, 4 * r:4 * r + 4], T.bli[:, 4 * r:4 * r + 4], k_bl)
-    d1 = tt(T.ps5[:, 0:256], T.nbi[:, 0:256], T.nbi[:, 256:512], A.subtract, k_nb)
+    b6 = cp(T.blh[:], T.bla[:], b4)
+    b7 = cp(T.bl15[:], T.blb[:], b5)
     d2 = tt(T.pf[:], T.wb[:, 0:256], T.wb[:, 256:512], A.is_ge, k_wb)
     d3 = tt(T.ps5[:, 256:512], T.pf[:], T.ps5[:, 0:256], A.mult, d2, d1)
     d4 = tt(T.u1f[:], T.nbi[:, 256:512], T.ps5[:, 256:512], A.add, d3)
@@ -205,10 +212,15 @@ def rank_program(g, core, T, topo):
                    T.we[:, 0:V].indirect(T.blgu[:, 4 * q:4 * q + 4]), float(2.0 ** (32 * (q - r))), None, A.mult,
                    deps=[b3] + k_we)
 
+    k_bm = None
+
+    def shown(out, tile, *deps):
+        return tt(out[:], tile.indirect(T.blh[:]), T.blm[:], A.mult, b6, k_bm, *deps)
+
     dma("y", "lx", T.xw[:, 0:V], T.x[:], [a_x0])
     k_x = dma("y", "lx", T.xc[:], T.x[:])
 
-    PARTS = [("v", 0, 64), ("a", 128, 64), ("v", 64, 64), ("a", 192, 64)]
+    PARTS = [("a", 144, 64), ("v", 0, 80), ("a", 208, 48), ("v", 80, 64)]
 
     def lookup(win, lst, deps, ps, gat, g0, sel, parts=PARTS, psdeps=()):
         tok = None
@@ -226,71 +238,81 @@ def rank_program(g, core, T, topo):
         return tok
 
     k_p1 = lookup(T.we, T.u1, k_we + [k_we2, k_u1], T.ps0, T.gat, 0, T.osel)
-    p1 = cp(T.p1b[:], T.ps0[:, 0:256], k_p1)
-    k_w1 = build(T.wp1, T.p1b, p1)
-    o1 = border("v", T.wp1, T.s1, b1, *k_w1)
-    a_x1 = exchange("x1", T.s1, slots, T.wp1, GO, o1)
-    z_1 = acp(T.wp1[:, GO[0]:GO[1]], T.s1[:, own[0]:own[1]], o1)
+    k_of = acp(T.oself[:], T.osel[:])
     e1 = tt(T.uof[:], T.nbi[:, 0:256], T.ps5[:, 256:512], A.subtract, d3)
+    k_bm = cp(T.blm[:], T.ohb[:].indirect(T.bl15[:]), b7, c7)
+    p1 = cp(T.p1b[:], T.ps0[:, 0:256], k_p1)
+    o1 = shown(T.s1, T.p1b[:], p1)
+    a_x1 = exchange("x1", T.s1, slots, T.wp, GO, o1)
+    k_r8 = dma("y", "lr8", T.r8[:], T.bo[0:128:16, :], [q_bo])
+    k_w1 = build(T.wp, T.p1b, p1)
     k_uo = cp(T.uo[:], T.uof[:], e1)
-    k_po = lookup(T.we, T.uo, k_we + [k_we2, k_uo], T.ps1, T.gat, 4096, T.osel)
-    k_lt1 = tt(T.lt1[:], T.p1b[:], T.eb[:], A.is_lt)
-    k_um = ts(T.tmp[:], T.u1f[:], float(-ZC), A.add, d4)
-    vx = op("v", g.vector.memset, T.xw[:, ZC:ZC + 16], 0.0)
-    vs = op("v", g.vector.memset, T.sw[:, ZC:ZC + 16], 0.0)
+    z_1 = acp(T.wp[:, GO[0]:GO[1]], T.s1[:, own[0]:own[1]], o1)
+    lookup(T.we, T.uo, k_we + [k_we2, k_uo], T.ps1, T.gat, V, T.osel, parts=[("v", 0, 64), ("a", 128, 64), ("a", 192, 64)])
+    k_um = ts(T.ps5[:, 256:512], T.u1f[:], float(-ZC), A.add, e1)
+    k_lt1 = tt(T.ps5[:, 0:256], T.ps0[:, 0:256], T.eb[:], A.is_lt)
 
-    k_r1 = lookup(T.wp1, T.u1, k_w1 + [a_x1, z_1], T.ps2, T.gat, 0, T.osel)
+    k_r1 = lookup(T.wp, T.u1, k_w1 + [a_x1, z_1], T.ps2, T.gat, 0, T.osel)
+    nbs = [shown(T["nbm%d" % d], T.nbi[:, 256 * d:256 * d + 256]) for d in range(2)]
     m1 = tt(T.m1[:], T.ps2[:, 0:256], T.eb[:], A.is_equal, k_r1)
-    k_wm = build(T.wm, T.m1, m1)
-    o2 = border("v", T.wm, T.s2, *k_wm)
+    o2 = shown(T.s2, T.m1[:], m1)
     a_x2 = exchange("x2", T.s2, slots, T.wm, GO, o2)
-    z_2 = acp(T.wm[:, GO[0]:GO[1]], T.s2[:, own[0]:own[1]], o2)
     for c in range(16):
         k_wr = dma("y", "lwr", T.wr0[c:128:16, :], T.w[:, 0:V], [a_x1])
     k_w8 = dma("y", "lw8", T.w8[:], T.w[:, V:2 * V])
-    ox = border("v", T.xw, T.sx, k_x)
+    for d in range(2):
+        wait("t", [nbs[d], k_of])
+        for c in range(16):
+            args = (T.ps6[:, 16 * d:16 * d + 16], T.oself[:, 128 * c:128 * c + 128], T["nbm%d" % d][:, c:256:16], c == 0, c == 15)
+            if c < 15:
+                g.tensor.matmul(*args)
+            else:
+                k_nm = op("t", g.tensor.matmul, *args)
+    k_wm = build(T.wm, T.m1, m1)
+    z_2 = acp(T.wm[:, GO[0]:GO[1]], T.s2[:, own[0]:own[1]], o2)
+    k_po = lookup(T.we, T.uo, k_we + [k_we2, k_uo], T.ps1, T.gat, V, T.osel, parts=[("a", 64, 64)])
+    ox = border(T.xw, T.sx, k_x, b1)
     a_xx = exchange("xx", T.sx, slots, T.xw, GO, ox)
     z_x = acp(T.xw[:, GO[0]:GO[1]], T.sx[:, own[0]:own[1]], ox)
     q_y1 = op("g", g.iota, T.yb[:, DUMP:DUMP + V // 2], [[0, V // 2]], 0, 0, allow_small_or_imprecise_dtypes=True)
-    k_nr1 = tt(T.nr1[:], T.m1[:], T.lt1[:], A.mult, k_lt1)
-    f1 = tt(T.tm2[:], T.m1[:], T.tmp[:], A.mult, k_um)
-    k_d = tt(T.dif[:], T.u1f[:], T.uof[:], A.subtract, e1)
+    f1 = tt(T.tm2[:], T.m1[:], T.ps5[:, 256:512], A.mult, k_um)
+    k_nr1 = tt(T.nr1[:], T.m1[:], T.ps5[:, 0:256], A.mult, k_lt1)
+    vx = op("v", g.vector.memset, T.xw[:, ZC:ZC + 16], 0.0)
+    vs = op("v", g.vector.memset, T.sw[:, ZC:ZC + 16], 0.0)
+    c8 = ts(T.gco2[:, 0:1], T.gcol[:, 0:1], float(4096 * r - DUMP), A.add)
+    k_vb = plus(T.ps7[:, 0:256], T.ivb[:], T.gcol[:, 0:1], q_vb, eb)
+    k_dm = plus(T.dm[:], T.idm[:], T.gcol[:, 0:1], q_dm)
+    k_dmo = plus(T.dmo[:], T.idm[:], T.gco2[:, 0:1], c8)
 
     k_a1 = lookup(T.wm, T.u1, k_wm + [a_x2, z_2], T.ps3, T.gat, 0, T.osel)
-    k_ao = lookup(T.wm, T.uo, k_wm + [a_x2, z_2], T.ps4, T.gat, 4096, T.osel)
+    k_ao = lookup(T.wm, T.uo, k_wm + [a_x2, z_2, k_po], T.ps4, T.gat, V, T.osel)
     h1 = ts(T.z1[:], T.ps3[:, 0:256], 0.0, A.is_equal, k_a1)
+    k_d = tt(T.ps2[:, 256:512], T.u1f[:], T.uof[:], A.subtract)
     h2 = tt(T.ps5[:, 0:256], T.z1[:], T.ps0[:, 0:256], A.mult, h1)
     h3 = tt(T.ps5[:, 256:512], T.m1[:], T.ps4[:, 0:256], A.add, k_ao)
     h4 = tt(T.t2[:], T.z1[:], T.ps5[:, 256:512], A.add, h3)
     h5 = ts(T.cq[:], T.t2[:], 0.0, A.is_equal, h4)
     h6 = tt(T.bq[:], T.cq[:], T.ps1[:, 0:256], A.mult, h5, k_po)
     p2 = tt(T.p2b[:], T.bq[:], T.ps5[:, 0:256], A.add, h6, h2)
-    k_w2 = build(T.wp2, T.p2b, p2)
-    o3 = border("v", T.wp2, T.s3, *k_w2)
-    a_x3 = exchange("x3", T.s3, slots, T.wp2, GO, o3)
-    z_3 = acp(T.wp2[:, GO[0]:GO[1]], T.s3[:, own[0]:own[1]], o3)
+    o3 = shown(T.s3, T.p2b[:], p2)
+    a_x3 = exchange("x3", T.s3, slots, T.wp, GO, o3)
+    k_w2 = build(T.wp, T.p2b, p2, nv=8)
+    z_3 = acp(T.wp[:, GO[0]:GO[1]], T.s3[:, own[0]:own[1]], o3)
     q_y2 = op("g", g.iota, T.yb[:, DUMP + V // 2:DUMP + V], [[0, V // 2]], 0, 0, allow_small_or_imprecise_dtypes=True)
-    i1 = tt(T.tmp[:], T.z1[:], T.dif[:], A.mult, k_d, f1)
-    k_A = ts(T.ps5[:, 256:512], T.tm2[:], float(ZC), A.add, f1)
-    i2 = tt(T.u2f[:], T.uof[:], T.tmp[:], A.add, i1)
-    k_lt2 = tt(T.lt2[:], T.p2b[:], T.eb[:], A.is_lt, p2)
+    i1 = tt(T.ps2[:, 256:512], T.z1[:], T.ps2[:, 256:512], A.mult, k_d)
+    k_nbb = cp(T.nbb[:], T.ps6[:, 0:32], k_nm)
+    i2 = tt(T.u2f[:], T.uof[:], T.ps2[:, 256:512], A.add, i1)
+    k_lt2 = tt(T.ps6[:, 256:512], T.p2b[:], T.eb[:], A.is_lt, k_nbb)
     k_u2 = cp(T.u2[:], T.u2f[:], i2)
-    k_B = ts(T.ps5[:, 0:256], T.u2f[:], float(-ZC), A.add, i2, p2)
-    k_nbu = cp(T.nbu[:], T.nbi[:])
-    n1 = op("v", g.vector.tensor_scalar, T.ntt[:], T.itri[:], 0, -1.0, A.is_le, A.mult, deps=[q_tri])
-    n3 = ts(T.ira[:], T.ir8[:], 4, A.arith_shift_right, q_r8)
-    n5 = ts(T.vb[:], T.ivb[:], T.gcol[:, 0:1], A.add, q_vb)
-    n6 = ts(T.dm[:], T.idm[:], T.gcol[:, 0:1], A.add, q_dm)
-    n2 = tt(T.nt[:], T.ntt[:], T.bo[:], A.mult, n1, k_bo)
-    n4 = ts(T.r8[:], T.ira[:], 0, A.is_equal, n3)
-    n7 = ts(T.dmo[:], T.dm[:], float(4096 * r - DUMP), A.add, n6)
-    n8 = ts(T.idn[:], T.itri[:], 0, A.is_equal)
-    k_of = acp(T.oself[:], T.osel[:])
+    k_A = plus(T.ps1[:, 256:512], T.tm2[:], float(ZC), f1, p2)
+    k_B = plus(T.ps1[:, 0:256], T.u2f[:], float(-ZC), i2)
 
-    k_r2 = lookup(T.wp2, T.u2, k_w2 + [a_x3, z_3, k_u2], T.ps2, T.gat, 0, T.osel)
+    k_r2 = lookup(T.wp, T.u2, k_w2 + [a_x3, z_3, k_u2], T.ps2, T.gat, 0, T.osel)
+    y0 = shown(T.wbm0, T.wb[:, 0:256])
+    y1 = shown(T.wbm1, T.wb[:, 256:512])
     m2 = tt(T.m2[:], T.ps2[:, 0:256], T.eb[:], A.is_equal, k_r2)
-    j1 = tt(T.tmp[:], T.m2[:], T.ps5[:, 0:256], A.mult, m2, k_B)
-    j2 = tt(T.mof[:], T.tmp[:], T.ps5[:, 256:512], A.add, j1, k_A)
+    j1 = tt(T.tmp[:], T.m2[:], T.ps1[:, 0:256], A.mult, m2, k_B)
+    j2 = tt(T.mof[:], T.tmp[:], T.ps1[:, 256:512], A.add, j1, k_A)
     k_mo = cp(T.mo[:], T.mof[:], j2)
 
     NC = V // CH
@@ -303,57 +325,66 @@ def rank_program(g, core, T, topo):
     for j in range(3):
         sl = slice(FD + CH * j, FD + CH * (j + 1))
         gx.append(acp(T.gat[:, sl], T.xw[:].indirect(T.mo[:, (FD + CH * j) // 16:(FD + CH * (j + 1)) // 16]), *dep_x))
-        wait("t", [n8, k_x, p2])
+        wait("t", [q_id, k_x, p2])
         g.tensor.matmul(banks[j][:], T.idn[:], T.xc[:, sl], True, False)
         px.append(op("t", g.tensor.matmul, banks[j][:], T.idn[:], T.gat[:, sl], False, True, deps=[gx[j]]))
         if j >= 1:
             k_fa = acp(T.fx[:, FD + CH * (j - 1):FD + CH * j], banks[j - 1][:], px[j - 1])
     k_fa = acp(T.fx[:, FD + 2 * CH:V], banks[2][:], px[2])
-    o4 = border("v", T.fx, T.s4, k_fv, k_fa)
+    r1 = tt(T.ps5[:, 0:256], T.m2[:], T.ps6[:, 256:512], A.mult, k_lt2, j2)
+    o4 = border(T.fx, T.s4, k_fv, k_fa)
     a_x4 = exchange("x4", T.s4, slots, T.fx, GO, o4)
+    op("t", g.tensor.matmul, T.ps4[:, 0:256], T.bo[:], T.wbm0[:], True, True, deps=[y0, y1, q_bo])
+    k_pw = op("t", g.tensor.matmul, T.ps4[:, 256:512], T.bo[:], T.wbm1[:], True, True)
     z_4 = acp(T.fx[:, GO[0]:GO[1]], T.s4[:, own[0]:own[1]], o4)
+    k_ws = acp(T.wbs[:], T.ps4[:], k_pw)
 
-    r1 = tt(T.nr2[:], T.m2[:], T.lt2[:], A.mult, k_lt2)
-    r2 = tt(T.nr[:], T.nr2[:], T.nr1[:], A.add, r1, k_nr1)
+    r2 = tt(T.nr[:], T.nr1[:], T.ps5[:, 0:256], A.add, r1, k_nr1)
+    l1 = tt(T.ps5[:, 256:512], T.mof[:], T.ps7[:, 0:256], A.subtract, k_vb)
     k_rep = ts(T.rep[:], T.nr[:], 0.0, A.is_equal, r2)
-    op("t", g.tensor.matmul, T.ps6[:, 0:256], T.bo[:], T.rep[:], True, True, deps=[k_rep, k_bo])
-    k_pn = op("t", g.tensor.matmul, T.ps6[:, 256:512], T.nt[:], T.rep[:], True, True, deps=[n2])
-    l1 = tt(T.tmp[:], T.mof[:], T.vb[:], A.subtract, n5)
+    op("t", g.tensor.matmul, T.ps6[:, 0:256], T.bo[:], T.rep[:], True, True, deps=[k_rep])
+    k_pn = op("t", g.tensor.matmul, T.ps6[:, 256:512], T.nt[:], T.rep[:], True, True, deps=[q_nt])
+    l2 = tt(T.dif[:], T.nr[:], T.ps5[:, 256:512], A.mult, l1)
+    k_nbu = cp(T.nbu[:], T.nbi[:])
     k_in = op("v", g.vector.tensor_tensor_scan, T.inc[:], T.ps6[:, 0:256], T.zz[:], float(4096 * r), A.add, A.add, deps=[k_pn])
-    l2 = tt(T.tm2[:], T.nr[:], T.tmp[:], A.mult, l1, k_A)
-    k_num = tt(T.num[:], T.inc[:], T.ps6[:, 256:512], A.add, k_in)
-    l3 = tt(T.dif[:], T.tm2[:], T.vb[:], A.add, l2)
-    l4 = tt(T.uof[:], T.num[:], T.dmo[:], A.subtract, k_num, n7)
-    k_cl = cp(T.cl[:], T.dif[:], l3)
-    l5 = tt(T.mant[:], T.uof[:], T.rep[:], A.mult, l4)
-    l6 = tt(T.inc[:], T.mant[:], T.dm[:], A.add, l5, k_num)
-    k_pos = cp(T.pos[:], T.inc[:], l6)
+    l3 = tt(T.tmp[:], T.dif[:], T.ps7[:, 0:256], A.add, l2)
+    k_num = tt(T.num[:], T.inc[:], T.ps6[:, 256:512], A.subtract, k_in)
+    k_cl = cp(T.cl[:], T.tmp[:], l3)
+    o6 = shown(T.s6, T.num[:], k_num)
+    a_x6 = exchange("x6", T.s6, slots, T.wn, GO, o6)
+    k_wn = build(T.wn, T.num, k_num, nv=0, blocks=range(8))
 
     dep_f = [k_fv, k_fa, a_x4, z_4]
+    tb = [tt(T["tb%d" % d][:], T.fx[:].indirect(T.nbb[:, 16 * d:16 * d + 16]), T.wbs[:, 256 * d:256 * d + 256], A.mult, k_nbb, k_ws, *dep_f)
+          for d in range(2)]
     t0, mm, ss, gg, pw = {}, {}, {}, {}, {}
     for i in range(NC + 2):
+        if i == 2:
+            k_wn = build(T.wn, T.num, k_num, nv=0, blocks=range(8, 16))
+            z_6 = acp(T.wn[:, GO[0]:GO[1]], T.s6[:, own[0]:own[1]], o6)
         if i < NC:
             sl = slice(CH * i, CH * i + CH)
             gg[i] = acp(T.g1[:, sl], T.fx[:].indirect(T.nbu[:, 256 + KC * i:256 + KC * (i + 1)]), k_nbu, *dep_f)
-            pw[i] = op("t", g.tensor.matmul, T["ps%d" % (i % 2)][:], T.r8[:], T.w8[:, sl], True, True, deps=[n4, k_w8, k_fa, mm.get(i - 2)])
+            pw[i] = op("t", g.tensor.matmul, T["ps%d" % (i % 2)][:], T.r8[:], T.w8[:, sl], True, True, deps=[k_r8, k_w8, k_fa, mm.get(i - 2)])
             t0[i] = tt(T.sw[:, sl], T.fx[:].indirect(T.nbu[:, KC * i:KC * (i + 1)]), T.wr0[:, sl], A.mult, k_wr, *dep_f)
+        if i == 0:
+            o5 = tt(T.s5[:], T.tb0[:], T.tb1[:], A.add, *tb)
+            a_x5 = exchange("x5", T.s5, slots, T.sw, GO, o5)
         if 0 <= i - 1 < NC:
             k = i - 1
             sl = slice(CH * k, CH * k + CH)
-            mm[k] = tt(T["ps%d" % (2 + k % 3)][:], T.g1[:, sl], T["ps%d" % (k % 2)][:], A.mult, gg[k], pw[k], ss.get(k - 3))
+            mm[k] = tt(T["ps%d" % (2 + k % 3)][:], T.g1[:, sl], T["ps%d" % (k % 2)][:], A.mult, gg[k], pw[k], k_ws, ss.get(k - 3))
         if 0 <= i - 2 < NC:
             k = i - 2
             sl = slice(CH * k, CH * k + CH)
             ss[k] = tt(T.sw[:, sl], T.sw[:, sl], T["ps%d" % (2 + k % 3)][:], A.add, t0[k], mm[k])
 
-    k_wn = build(T.wn, T.num, k_num, nv=0)
-    o6 = border("a", T.wn, T.s6, *k_wn)
-    a_x6 = exchange("x6", T.s6, slots, T.wn, GO, o6)
-    z_6 = acp(T.wn[:, GO[0]:GO[1]], T.s6[:, own[0]:own[1]], o6)
-    o5 = border("v", T.sw, T.s5, ss[NC - 1])
-    a_x5 = exchange("x5", T.s5, slots, T.sw, GO, o5)
     z_5 = acp(T.sw[:, GO[0]:GO[1]], T.s5[:, own[0]:own[1]], o5)
-    k_cm = lookup(T.wn, T.cl, k_wn + [a_x6, z_6, k_cl], T.ps7, T.gatn, 0, T.oself, psdeps=[k_of])
+    k_cm = lookup(T.wn, T.cl, k_wn + [a_x6, z_6, k_cl], T.ps7, T.gatn, 0, T.oself, parts=[("a", 64 * j, 64) for j in range(4)], psdeps=[k_of, l3])
+    l4 = tt(T.ps5[:, 0:256], T.num[:], T.dmo[:], A.subtract, k_dmo)
+    l5 = tt(T.mant[:], T.rep[:], T.ps5[:, 0:256], A.mult, l4)
+    l6 = tt(T.inc[:], T.mant[:], T.dm[:], A.add, l5, k_dm)
+    k_pos = cp(T.pos[:], T.inc[:], l6)
 
     w = None
     for i in range(NC - 1, -1, -1):

@@ -7,6 +7,8 @@ GH = V + N * C
 ZC = GH
 CH = 512
 DUMP = 512
+DMA_CHUNKS = (0, 1, 2)
+NV = 8
 
 SCRATCH = {}
 
@@ -24,8 +26,8 @@ _declare("nbu", 512, "uint16")
 _declare("z", (2, 16, 16), "bfloat16")
 _declare("wb wbs", 512, "bfloat16")
 _declare("u1 uo u2 mo pos cl", 256, "uint16")
-_declare("u1f uof u2f dif tmp tm2 mof num inc cms ivb idm dm dmo fd zz mant s4 s5 s6 nbm0 nbm1 tb0 tb1", 256, "float32")
-_declare("pf p1b p2b m1 m2 nr1 nr rep z1 t2 cq bq eb s1 s2 s3 sx blm wbm0 wbm1", 256, "bfloat16")
+_declare("u1f uof u2f dif tmp tm2 mof num inc cms ivb idm fd zz mant s4 s5 s6 nbm0 nbm1 tb0 tb1", 256, "float32")
+_declare("pf p1b p2b m1 m2 nr1 nr rep z1 fr sg b0 bz eb ebf s1 s2 s3 sx blm wbm0 wbm1", 256, "bfloat16")
 _declare("im", 256, "int32")
 _declare("ohf", 16, "float32")
 _declare("ohb", 16, "bfloat16")
@@ -50,7 +52,7 @@ for _i in range(8):
     SCRATCH["ps%d" % _i] = ("psum", [128, 512], "float32")
 
 EXCH = ["x0", "x1", "x2", "xx", "x3", "x4", "x6", "x5"]
-LOADS = ["lbl", "lnb", "lw", "lx", "lwr", "lw8", "lr8", "sty", "stc"]
+LOADS = ["lbl", "lnb", "lw", "lx", "lwr", "lw8", "lr8", "sty", "stc"] + ["ad%d" % k for k in DMA_CHUNKS]
 SEMAPHORES = ["v", "a", "t", "q", "sent"] + EXCH + LOADS
 
 
@@ -97,9 +99,9 @@ def rank_program(g, core, T, topo):
         cnt[SEM[qn]] += 1
         return (SEM[qn], cnt[SEM[qn]])
 
-    def dma(qn, sem, out, in_, deps=()):
+    def dma(qn, sem, out, in_, deps=(), **kw):
         wait(qn, deps)
-        Q[qn].dma_start(out, in_).then_inc(T.sem[sem], 16)
+        Q[qn].dma_start(out, in_, **kw).then_inc(T.sem[sem], 16)
         cnt[sem] += 16
         return (sem, cnt[sem])
 
@@ -115,8 +117,8 @@ def rank_program(g, core, T, topo):
     def acp(o, a, *deps, **kw):
         return op("a", g.scalar.activation, o, a, COPY, deps=deps, **kw)
 
-    def plus(o, a, b, *deps):
-        return op("a", g.scalar.activation, o, a, IDENT, bias=b, deps=deps)
+    def plus(o, a, b, *deps, **kw):
+        return op("a", g.scalar.activation, o, a, IDENT, bias=b, deps=deps, **kw)
 
     mine = link_engines(topo, cores, core)
 
@@ -143,9 +145,6 @@ def rank_program(g, core, T, topo):
     own = slots(r)
     GO = (V + C * r, V + C * r + C)
 
-    def border(buf, snd, *deps):
-        return cp(snd[:], buf[:, 0:V].indirect(T.blu[:]), *deps)
-
     k_bl = dma("y", "lbl", T.bli[:], T.bl[:])
     k_nb = dma("y", "lnb", T.nbi[:], T.nb[:])
     dma("a", "lw", T.z[:, 0], T.w[0::2, :])
@@ -164,10 +163,11 @@ def rank_program(g, core, T, topo):
     q_id = op("g", g.affine_select, T.idn[:], T.bo[:], [[-1, 128]], A.is_equal, 0.0, 0, 1, deps=[q_bo])
 
     v0 = op("v", g.vector.memset, T.zz[:], 0.0)
-    v1 = op("v", g.vector.memset, T.fd[:], 1.0)
+    a0 = op("v", g.vector.memset, T.osel[:, 0:1024], 0.0)
     c1 = ts(T.iga[:], T.igh[:], 4, A.arith_shift_right, q_gh)
-    v2 = op("v", g.vector.memset, T.fd[:, 8:256:8], 2.0, deps=[v1])
     c4 = ts(T.ghb[:], T.iga[:], 0, A.is_equal, c1)
+    v1 = op("v", g.vector.memset, T.fd[:], 1.0)
+    v2 = op("v", g.vector.memset, T.fd[:, 8:256:8], 2.0, deps=[v1])
     c2 = ts(T.icc[:, 0:1], T.igh[:, 0:1], 15, A.bitwise_and, q_gh)
     c3 = ts(T.ioa[:], T.ioh[:], 15, A.bitwise_and, q_oh)
     fe = op("v", g.vector.tensor_tensor_scan, T.ps7[:, 0:256], T.fd[:], T.zz[:], float(2.0 ** (32 * r - 71)), A.mult, A.add, deps=[v2, v0])
@@ -177,12 +177,12 @@ def rank_program(g, core, T, topo):
     mt = ts(T.mant[:], T.im[:], T.gcol[:, 0:1], A.add, q_im, c5)
     eb = tt(T.eb[:], T.mant[:], T.ps7[:, 0:256], A.mult, mt, fe)
 
-    for c in range(8):
-        a0 = acp(T.osel[:, 256 * c:256 * c + 256], T.zz[:], v0)
+    for c in range(4, 8):
+        a1 = acp(T.osel[:, 256 * c:256 * c + 256], T.zz[:], v0)
     for c in range(16):
-        k_os = acp(T.osel[:, 129 * c:128 * (c + 1):16], T.ghb[:], c4, a0)
+        k_os = acp(T.osel[:, 129 * c:128 * (c + 1):16], T.ghb[:], c4, a0, a1)
 
-    def build(win, src, c_src, nv=10, blocks=range(16)):
+    def build(win, src, c_src, nv=NV, blocks=range(16)):
         tv = ta = None
         for c in blocks:
             if c < nv:
@@ -193,29 +193,29 @@ def rank_program(g, core, T, topo):
 
     k_we = build(T.we, T.eb, eb, nv=6)
 
-    d1 = tt(T.ps5[:, 0:256], T.nbi[:, 0:256], T.nbi[:, 256:512], A.subtract, k_nb)
     b1 = cp(T.blu[:], T.bli[:], k_bl)
     b2 = cp(T.blg[:, 4 * r:4 * r + 4], T.bli[:, 4 * r:4 * r + 4])
-    b4 = ts(T.bla[:], T.bli[:], 4, A.arith_shift_right)
-    b5 = ts(T.blb[:], T.bli[:], 15, A.bitwise_and)
     for b in range(16):
         k_wb = op("v", g.vector.transpose, T.wb[:, b:512:16], T.z[:, :, b, :], deps=[k_w])
-    b6 = cp(T.blh[:], T.bla[:], b4)
-    b7 = cp(T.bl15[:], T.blb[:], b5)
+    d1 = tt(T.ps5[:, 0:256], T.nbi[:, 0:256], T.nbi[:, 256:512], A.subtract, k_nb)
     d2 = tt(T.pf[:], T.wb[:, 0:256], T.wb[:, 256:512], A.is_ge, k_wb)
     d3 = tt(T.ps5[:, 256:512], T.pf[:], T.ps5[:, 0:256], A.mult, d2, d1)
     d4 = tt(T.u1f[:], T.nbi[:, 256:512], T.ps5[:, 256:512], A.add, d3)
     k_u1 = cp(T.u1[:], T.u1f[:], d4)
     b3 = cp(T.blgu[:], T.blg[:], a_x0, b2)
     for q in range(N):
-        k_we2 = op("v", g.vector.tensor_scalar, T.we[:, V + C * q:V + C * q + C],
-                   T.we[:, 0:V].indirect(T.blgu[:, 4 * q:4 * q + 4]), float(2.0 ** (32 * (q - r))), None, A.mult,
-                   deps=[b3] + k_we)
+        out, src = T.we[:, V + C * q:V + C * q + C], T.we[:, 0:V].indirect(T.blgu[:, 4 * q:4 * q + 4])
+        f = float(2.0 ** (32 * (q - r)))
+        if q < 2:
+            k_e1 = op("v", g.vector.tensor_scalar, out, src, f, None, A.mult, deps=[b3] + k_we)
+        else:
+            k_e2 = acp(out, src, b3, *k_we, scale=f)
+    k_we2 = k_we + [k_e1, k_e2]
 
-    k_bm = None
+    k_sh = []
 
     def shown(out, tile, *deps):
-        return tt(out[:], tile.indirect(T.blh[:]), T.blm[:], A.mult, b6, k_bm, *deps)
+        return tt(out[:], tile.indirect(T.blh[:]), T.blm[:], A.mult, *k_sh, *deps)
 
     dma("y", "lx", T.xw[:, 0:V], T.x[:], [a_x0])
     k_x = dma("y", "lx", T.xc[:], T.x[:])
@@ -237,10 +237,14 @@ def rank_program(g, core, T, topo):
                     tok = op("t", g.tensor.matmul, *args)
         return tok
 
-    k_p1 = lookup(T.we, T.u1, k_we + [k_we2, k_u1], T.ps0, T.gat, 0, T.osel)
+    k_p1 = lookup(T.we, T.u1, k_we2 + [k_u1], T.ps0, T.gat, 0, T.osel)
     k_of = acp(T.oself[:], T.osel[:])
     e1 = tt(T.uof[:], T.nbi[:, 0:256], T.ps5[:, 256:512], A.subtract, d3)
-    k_bm = cp(T.blm[:], T.ohb[:].indirect(T.bl15[:]), b7, c7)
+    b4 = ts(T.bla[:], T.bli[:], 4, A.arith_shift_right)
+    b5 = ts(T.blb[:], T.bli[:], 15, A.bitwise_and)
+    b6 = cp(T.blh[:], T.bla[:], b4)
+    b7 = cp(T.bl15[:], T.blb[:], b5)
+    k_sh += [b6, cp(T.blm[:], T.ohb[:].indirect(T.bl15[:]), b7, c7)]
     p1 = cp(T.p1b[:], T.ps0[:, 0:256], k_p1)
     o1 = shown(T.s1, T.p1b[:], p1)
     a_x1 = exchange("x1", T.s1, slots, T.wp, GO, o1)
@@ -248,7 +252,7 @@ def rank_program(g, core, T, topo):
     k_w1 = build(T.wp, T.p1b, p1)
     k_uo = cp(T.uo[:], T.uof[:], e1)
     z_1 = acp(T.wp[:, GO[0]:GO[1]], T.s1[:, own[0]:own[1]], o1)
-    lookup(T.we, T.uo, k_we + [k_we2, k_uo], T.ps1, T.gat, V, T.osel, parts=[("v", 0, 64), ("a", 128, 64), ("a", 192, 64)])
+    lookup(T.we, T.uo, k_we2 + [k_uo], T.ps1, T.gat, V, T.osel, parts=[("v", 0, 64), ("a", 128, 64)])
     k_um = ts(T.ps5[:, 256:512], T.u1f[:], float(-ZC), A.add, e1)
     k_lt1 = tt(T.ps5[:, 0:256], T.ps0[:, 0:256], T.eb[:], A.is_lt)
 
@@ -270,35 +274,33 @@ def rank_program(g, core, T, topo):
                 k_nm = op("t", g.tensor.matmul, *args)
     k_wm = build(T.wm, T.m1, m1)
     z_2 = acp(T.wm[:, GO[0]:GO[1]], T.s2[:, own[0]:own[1]], o2)
-    k_po = lookup(T.we, T.uo, k_we + [k_we2, k_uo], T.ps1, T.gat, V, T.osel, parts=[("a", 64, 64)])
-    ox = border(T.xw, T.sx, k_x, b1)
-    a_xx = exchange("xx", T.sx, slots, T.xw, GO, ox)
-    z_x = acp(T.xw[:, GO[0]:GO[1]], T.sx[:, own[0]:own[1]], ox)
-    q_y1 = op("g", g.iota, T.yb[:, DUMP:DUMP + V // 2], [[0, V // 2]], 0, 0, allow_small_or_imprecise_dtypes=True)
     f1 = tt(T.tm2[:], T.m1[:], T.ps5[:, 256:512], A.mult, k_um)
     k_nr1 = tt(T.nr1[:], T.m1[:], T.ps5[:, 0:256], A.mult, k_lt1)
-    vx = op("v", g.vector.memset, T.xw[:, ZC:ZC + 16], 0.0)
-    vs = op("v", g.vector.memset, T.sw[:, ZC:ZC + 16], 0.0)
-    c8 = ts(T.gco2[:, 0:1], T.gcol[:, 0:1], float(4096 * r - DUMP), A.add)
-    k_vb = plus(T.ps7[:, 0:256], T.ivb[:], T.gcol[:, 0:1], q_vb, eb)
-    k_dm = plus(T.dm[:], T.idm[:], T.gcol[:, 0:1], q_dm)
-    k_dmo = plus(T.dmo[:], T.idm[:], T.gco2[:, 0:1], c8)
+    k_po = lookup(T.we, T.uo, k_we2 + [k_uo], T.ps1, T.gat, V, T.osel, parts=[("v", 64, 64), ("a", 192, 64)])
 
     k_a1 = lookup(T.wm, T.u1, k_wm + [a_x2, z_2], T.ps3, T.gat, 0, T.osel)
-    k_ao = lookup(T.wm, T.uo, k_wm + [a_x2, z_2, k_po], T.ps4, T.gat, V, T.osel)
-    h1 = ts(T.z1[:], T.ps3[:, 0:256], 0.0, A.is_equal, k_a1)
+    k_fr = plus(T.fr[:], T.m1[:], 1.0, m1, scale=-1.0)
+    k_sg = plus(T.sg[:], T.m1[:], 1.0, scale=-2.0)
+    ox = acp(T.sx[:], T.xw[:, 0:V].indirect(T.blu[:]), k_x, b1)
+    a_xx = exchange("xx", T.sx, slots, T.xw, GO, ox)
+    z_x = acp(T.xw[:, GO[0]:GO[1]], T.sx[:, own[0]:own[1]], ox)
+    c8 = ts(T.gco2[:, 0:1], T.gcol[:, 0:1], float(4096 * r - DUMP), A.add)
+    k_vb = plus(T.ps7[:, 0:256], T.ivb[:], T.gcol[:, 0:1], q_vb, eb)
+    vx = op("v", g.vector.memset, T.xw[:, ZC:ZC + 16], 0.0)
+    vs = op("v", g.vector.memset, T.sw[:, ZC:ZC + 16], 0.0)
+    k_a0 = tt(T.ps5[:, 0:256], T.fr[:], T.ps0[:, 0:256], A.mult, k_fr, k_nr1)
+    k_ef = tt(T.ebf[:], T.eb[:], T.sg[:], A.mult, k_sg)
     k_d = tt(T.ps2[:, 256:512], T.u1f[:], T.uof[:], A.subtract)
-    h2 = tt(T.ps5[:, 0:256], T.z1[:], T.ps0[:, 0:256], A.mult, h1)
-    h3 = tt(T.ps5[:, 256:512], T.m1[:], T.ps4[:, 0:256], A.add, k_ao)
-    h4 = tt(T.t2[:], T.z1[:], T.ps5[:, 256:512], A.add, h3)
-    h5 = ts(T.cq[:], T.t2[:], 0.0, A.is_equal, h4)
-    h6 = tt(T.bq[:], T.cq[:], T.ps1[:, 0:256], A.mult, h5, k_po)
-    p2 = tt(T.p2b[:], T.bq[:], T.ps5[:, 0:256], A.add, h6, h2)
+    k_b0 = tt(T.b0[:], T.fr[:], T.ps1[:, 0:256], A.mult, k_po)
+    h1 = ts(T.z1[:], T.ps3[:, 0:256], 0.0, A.is_equal, k_a1)
+    h2 = tt(T.bz[:], T.b0[:], T.ps3[:, 0:256], A.mult, k_b0)
+    h3 = tt(T.ps5[:, 256:512], T.z1[:], T.ps5[:, 0:256], A.mult, h1, k_a0, f1)
+    p2 = tt(T.p2b[:], T.bz[:], T.ps5[:, 256:512], A.add, h2, h3)
     o3 = shown(T.s3, T.p2b[:], p2)
     a_x3 = exchange("x3", T.s3, slots, T.wp, GO, o3)
-    k_w2 = build(T.wp, T.p2b, p2, nv=8)
+    k_w2 = build(T.wp, T.p2b, p2)
     z_3 = acp(T.wp[:, GO[0]:GO[1]], T.s3[:, own[0]:own[1]], o3)
-    q_y2 = op("g", g.iota, T.yb[:, DUMP + V // 2:DUMP + V], [[0, V // 2]], 0, 0, allow_small_or_imprecise_dtypes=True)
+    q_y1 = op("g", g.iota, T.yb[:, DUMP:DUMP + V // 2], [[0, V // 2]], 0, 0, allow_small_or_imprecise_dtypes=True)
     i1 = tt(T.ps2[:, 256:512], T.z1[:], T.ps2[:, 256:512], A.mult, k_d)
     k_nbb = cp(T.nbb[:], T.ps6[:, 0:32], k_nm)
     i2 = tt(T.u2f[:], T.uof[:], T.ps2[:, 256:512], A.add, i1)
@@ -310,29 +312,30 @@ def rank_program(g, core, T, topo):
     k_r2 = lookup(T.wp, T.u2, k_w2 + [a_x3, z_3, k_u2], T.ps2, T.gat, 0, T.osel)
     y0 = shown(T.wbm0, T.wb[:, 0:256])
     y1 = shown(T.wbm1, T.wb[:, 256:512])
-    m2 = tt(T.m2[:], T.ps2[:, 0:256], T.eb[:], A.is_equal, k_r2)
+    m2 = tt(T.m2[:], T.ps2[:, 0:256], T.ebf[:], A.is_equal, k_r2, k_ef)
     j1 = tt(T.tmp[:], T.m2[:], T.ps1[:, 0:256], A.mult, m2, k_B)
     j2 = tt(T.mof[:], T.tmp[:], T.ps1[:, 256:512], A.add, j1, k_A)
     k_mo = cp(T.mo[:], T.mof[:], j2)
 
     NC = V // CH
     KC = CH // 16
-    FD = 5 * CH
+    CA = 448
+    FD = V - 3 * CA
     dep_x = [k_mo, k_x, a_xx, z_x, vx]
     k_fv = tt(T.fx[:, 0:FD], T.xw[:].indirect(T.mo[:, 0:FD // 16]), T.xc[:, 0:FD], A.add, *dep_x)
     banks = [T.ps0, T.ps1, T.ps3]
-    gx, px = [], []
-    for j in range(3):
-        sl = slice(FD + CH * j, FD + CH * (j + 1))
-        gx.append(acp(T.gat[:, sl], T.xw[:].indirect(T.mo[:, (FD + CH * j) // 16:(FD + CH * (j + 1)) // 16]), *dep_x))
+    sls = [slice(FD + CA * j, FD + CA * (j + 1)) for j in range(3)]
+    px = []
+    for j, sl in enumerate(sls):
+        gx = acp(T.gat[:, sl], T.xw[:].indirect(T.mo[:, sl.start // 16:sl.stop // 16]), *dep_x)
         wait("t", [q_id, k_x, p2])
-        g.tensor.matmul(banks[j][:], T.idn[:], T.xc[:, sl], True, False)
-        px.append(op("t", g.tensor.matmul, banks[j][:], T.idn[:], T.gat[:, sl], False, True, deps=[gx[j]]))
+        g.tensor.matmul(banks[j][:, 0:CA], T.idn[:], T.xc[:, sl], True, False)
+        px.append(op("t", g.tensor.matmul, banks[j][:, 0:CA], T.idn[:], T.gat[:, sl], False, True, deps=[gx]))
         if j >= 1:
-            k_fa = acp(T.fx[:, FD + CH * (j - 1):FD + CH * j], banks[j - 1][:], px[j - 1])
-    k_fa = acp(T.fx[:, FD + 2 * CH:V], banks[2][:], px[2])
+            k_fa = acp(T.fx[:, sls[j - 1]], banks[j - 1][:, 0:CA], px[j - 1])
+    k_fa = acp(T.fx[:, sls[2]], banks[2][:, 0:CA], px[2])
     r1 = tt(T.ps5[:, 0:256], T.m2[:], T.ps6[:, 256:512], A.mult, k_lt2, j2)
-    o4 = border(T.fx, T.s4, k_fv, k_fa)
+    o4 = cp(T.s4[:], T.fx[:, 0:V].indirect(T.blu[:]), k_fv, k_fa)
     a_x4 = exchange("x4", T.s4, slots, T.fx, GO, o4)
     op("t", g.tensor.matmul, T.ps4[:, 0:256], T.bo[:], T.wbm0[:], True, True, deps=[y0, y1, q_bo])
     k_pw = op("t", g.tensor.matmul, T.ps4[:, 256:512], T.bo[:], T.wbm1[:], True, True)
@@ -357,9 +360,9 @@ def rank_program(g, core, T, topo):
     dep_f = [k_fv, k_fa, a_x4, z_4]
     tb = [tt(T["tb%d" % d][:], T.fx[:].indirect(T.nbb[:, 16 * d:16 * d + 16]), T.wbs[:, 256 * d:256 * d + 256], A.mult, k_nbb, k_ws, *dep_f)
           for d in range(2)]
-    t0, mm, ss, gg, pw = {}, {}, {}, {}, {}
+    t0, mm, ss, gg, pw, free = {}, {}, {}, {}, {}, {}
     for i in range(NC + 2):
-        if i == 2:
+        if i == NC:
             k_wn = build(T.wn, T.num, k_num, nv=0, blocks=range(8, 16))
             z_6 = acp(T.wn[:, GO[0]:GO[1]], T.s6[:, own[0]:own[1]], o6)
         if i < NC:
@@ -370,28 +373,41 @@ def rank_program(g, core, T, topo):
         if i == 0:
             o5 = tt(T.s5[:], T.tb0[:], T.tb1[:], A.add, *tb)
             a_x5 = exchange("x5", T.s5, slots, T.sw, GO, o5)
-        if 0 <= i - 1 < NC:
-            k = i - 1
+        k = i - 1
+        if 0 <= k < NC:
             sl = slice(CH * k, CH * k + CH)
-            mm[k] = tt(T["ps%d" % (2 + k % 3)][:], T.g1[:, sl], T["ps%d" % (k % 2)][:], A.mult, gg[k], pw[k], k_ws, ss.get(k - 3))
-        if 0 <= i - 2 < NC:
-            k = i - 2
+            dst = T.g1[:, sl] if k in DMA_CHUNKS else T["ps%d" % (2 + k % 3)][:]
+            mm[k] = tt(dst, T.g1[:, sl], T["ps%d" % (k % 2)][:], A.mult, gg[k], pw[k], k_ws, free.get(k - 3))
+            if k in DMA_CHUNKS:
+                ss[k] = dma("g", "ad%d" % k, T.sw[:, sl], T.g1[:, sl], [t0[k], mm[k]], accum_op=A.add)
+        k = i - 2
+        if 0 <= k < NC and k not in DMA_CHUNKS:
             sl = slice(CH * k, CH * k + CH)
-            ss[k] = tt(T.sw[:, sl], T.sw[:, sl], T["ps%d" % (2 + k % 3)][:], A.add, t0[k], mm[k])
+            ss[k] = free[k] = tt(T.sw[:, sl], T.sw[:, sl], T["ps%d" % (2 + k % 3)][:], A.add, t0[k], mm[k])
+    q_y2 = op("g", g.iota, T.yb[:, DUMP + V // 2:DUMP + V], [[0, V // 2]], 0, 0, allow_small_or_imprecise_dtypes=True)
 
+    k_dm = plus(T.ps6[:, 0:256], T.idm[:], T.gcol[:, 0:1], q_dm, k_num)
+    k_dmo = plus(T.ps6[:, 256:512], T.idm[:], T.gco2[:, 0:1], c8)
     z_5 = acp(T.sw[:, GO[0]:GO[1]], T.s5[:, own[0]:own[1]], o5)
-    k_cm = lookup(T.wn, T.cl, k_wn + [a_x6, z_6, k_cl], T.ps7, T.gatn, 0, T.oself, parts=[("a", 64 * j, 64) for j in range(4)], psdeps=[k_of, l3])
-    l4 = tt(T.ps5[:, 0:256], T.num[:], T.dmo[:], A.subtract, k_dmo)
+
+    def coarse(parts):
+        return lookup(T.wn, T.cl, k_wn + [a_x6, z_6, k_cl], T.ps7, T.gatn, 0, T.oself, parts=[("a", 64 * j, 64) for j in parts], psdeps=[k_of, l3])
+
+    coarse((0, 1))
+    l4 = tt(T.ps5[:, 0:256], T.num[:], T.ps6[:, 256:512], A.subtract, k_dmo)
     l5 = tt(T.mant[:], T.rep[:], T.ps5[:, 0:256], A.mult, l4)
-    l6 = tt(T.inc[:], T.mant[:], T.dm[:], A.add, l5, k_dm)
+    l6 = tt(T.inc[:], T.mant[:], T.ps6[:, 0:256], A.add, l5, k_dm)
     k_pos = cp(T.pos[:], T.inc[:], l6)
 
     w = None
-    for i in range(NC - 1, -1, -1):
-        sl = slice(CH * i, CH * i + CH)
-        x = acp(T.g1[:, sl], T.sw[:].indirect(T.mo[:, KC * i:KC * (i + 1)]), a_x5, z_5, vs, mm[NC - 1], k_mo, ss[NC - 1])
-        w = tt(T.yb[:, 0:DUMP + CH * (i + 1)].indirect(T.pos[:, KC * i:KC * (i + 1)]), T.sw[:, sl], T.g1[:, sl], A.add, x, w, k_pos, q_y1, q_y2)
-        k_y = dma("y", "sty", T.y[:, sl], T.yb[:, DUMP + CH * i:DUMP + CH * (i + 1)], [w])
+    cuts = [CH * i for i in range(NC, 0, -1)] + [128, 0]
+    for n, (hi, lo) in enumerate(zip(cuts, cuts[1:])):
+        sl = slice(lo, hi)
+        x = acp(T.g1[:, sl], T.sw[:].indirect(T.mo[:, lo // 16:hi // 16]), a_x5, z_5, vs, mm[NC - 1], k_mo, *ss.values())
+        w = tt(T.yb[:, 0:DUMP + hi].indirect(T.pos[:, lo // 16:hi // 16]), T.sw[:, sl], T.g1[:, sl], A.add, x, w, k_pos, q_y1, q_y2, *ss.values())
+        k_y = dma("y", "sty", T.y[:, sl], T.yb[:, DUMP + lo:DUMP + hi], [w])
+        if n in (2, 4):
+            k_cm = coarse((2 + n // 4,))
     k_c = acp(T.cms[:], T.ps7[:, 0:256], k_cm)
     k_st = dma("y", "stc", T.cm[:], T.cms[:], [k_c])
     wait("y", [(s, cnt[s]) for s in SEMAPHORES if cnt[s]])

import numpy as np
from concourse.bass import DstId, RemoteDMATransfer
from concourse.mybir import AluOpType, ActivationFunctionType

V, C, N = 4096, 64, 4
GH = V + N * C
ZC = GH
CH = 512
DUMP = 512
DMA_CHUNKS = (0, 1, 2)
NV = 8

SCRATCH = {}


def _declare(names, cols, dtype, rows=128):
    for n in names.split():
        SCRATCH[n] = ("sbuf", [rows, cols] if isinstance(cols, int) else [rows] + list(cols), dtype)


_declare("bli blg ioh ioa bla blb", 16, "int32")
_declare("blu blgu blh bl15", 16, "uint16")
_declare("nbb", 32, "uint16")
_declare("nbi", 512, "int32")
_declare("nbu", 512, "uint16")
_declare("z", (2, 16, 16), "bfloat16")
_declare("wb wbs", 512, "bfloat16")
_declare("u1 uo u2 mo pos cl", 256, "uint16")
_declare("u1f uof u2f dif tmp tm2 mof num inc cms ivb idm fd zz mant s4 s5 s6 nbm0 nbm1 tb0 tb1", 256, "float32")
_declare("pf p1b p2b m1 m2 nr1 nr rep z1 fr sg b0 bz eb ebf s1 s2 s3 sx blm wbm0 wbm1", 256, "bfloat16")
_declare("im", 256, "int32")
_declare("ohf", 16, "float32")
_declare("ohb", 16, "bfloat16")
_declare("igh iga", 8, "int32")
_declare("ghb", 8, "bfloat16")
_declare("icc", 2, "int32")
_declare("gcol gco2", 2, "float32")
_declare("r8", 128, "bfloat16", 8)
_declare("osel", 2048, "bfloat16")
_declare("oself", 2048, "float32")
_declare("bo nt idn", 128, "bfloat16")
_declare("we wp wm", GH, "bfloat16")
_declare("wn fx", GH, "float32")
_declare("gat", 2 * V, "bfloat16")
_declare("gatn g1", V, "float32")
_declare("xc wr0", V, "bfloat16")
_declare("xw", GH + 16, "bfloat16")
_declare("sw", GH + 16, "float32")
_declare("w8", V, "bfloat16", 8)
_declare("yb", DUMP + V, "float32")
for _i in range(8):
    SCRATCH["ps%d" % _i] = ("psum", [128, 512], "float32")

EXCH = ["x0", "x1", "x2", "xx", "x3", "x4", "x6", "x5"]
LOADS = ["lbl", "lnb", "lw", "lx", "lwr", "lw8", "lr8", "sty", "stc"] + ["ad%d" % k for k in DMA_CHUNKS]
SEMAPHORES = ["v", "a", "t", "q", "sent"] + EXCH + LOADS


def link_engines(topo, cores, src):
    on = [d for d in cores if d != src and topo.chip(d) == topo.chip(src)]
    off = [d for d in cores if d != src and topo.chip(d) != topo.chip(src)]
    out, used = {}, []
    for d in off + on:
        left = [e for e in topo.engines(src, d) if e not in used]
        if d in on and off:
            far = topo.engines(src, off[0])
            left = [e for e in left if e not in far] or left
        out[d] = left[:4]
        used += out[d]
    return out


def rank_program(g, core, T, topo):
    r = T.rank_of(core)
    if r is None:
        return
    A = AluOpType
    COPY = ActivationFunctionType.Copy
    IDENT = ActivationFunctionType.Identity
    cores = list(T.cores)
    Q = {"v": g.vector, "a": g.scalar, "t": g.tensor, "g": g, "y": g.sync}
    SEM = {"v": "v", "a": "a", "t": "t", "g": "q"}
    cnt = {s: 0 for s in SEMAPHORES}
    seen = {}

    def wait(qn, deps):
        best = {}
        for d in deps:
            if d is not None:
                best[d[0]] = max(best.get(d[0], 0), d[1])
        for s, n in best.items():
            if seen.get((qn, s), 0) < n:
                Q[qn].wait_ge(T.sem[s], n)
                seen[(qn, s)] = n

    def op(qn, fn, *args, deps=(), **kw):
        wait(qn, deps)
        fn(*args, **kw).then_inc(T.sem[SEM[qn]], 1)
        cnt[SEM[qn]] += 1
        return (SEM[qn], cnt[SEM[qn]])

    def dma(qn, sem, out, in_, deps=(), **kw):
        wait(qn, deps)
        Q[qn].dma_start(out, in_, **kw).then_inc(T.sem[sem], 16)
        cnt[sem] += 16
        return (sem, cnt[sem])

    def tt(o, a, b, f, *deps):
        return op("v", g.vector.tensor_tensor, o, a, b, f, deps=deps)

    def ts(o, a, s1, f, *deps):
        return op("v", g.vector.tensor_scalar, o, a, s1, None, f, deps=deps)

    def cp(o, a, *deps):
        return op("v", g.vector.tensor_copy, o, a, deps=deps)

    def acp(o, a, *deps, **kw):
        return op("a", g.scalar.activation, o, a, COPY, deps=deps, **kw)

    def plus(o, a, b, *deps, **kw):
        return op("a", g.scalar.activation, o, a, IDENT, bias=b, deps=deps, **kw)

    mine = link_engines(topo, cores, core)

    def exchange(sem, src, piece, dst, place, *deps):
        wait("g", deps)
        tr = []
        for q in range(N):
            if q == r:
                continue
            d = cores[q]
            a = topo.addr(d)
            a0, a1 = piece(q)
            tr.append(RemoteDMATransfer(dst_ids=[DstId(rid=a[0], pnc=a[1])],
                                        dma_engine_mask=sum(1 << e for e in mine[d]), remote_sem=T.sem[sem],
                                        srcs=[src[:, a0:a1]], dsts=[dst[:, place[0]:place[1]]]))
        g.remote_dma_fused(tr, local_sem=T.sem.sent)
        cnt["sent"] += sum(len(mine[d]) for d in mine)
        cnt[sem] += sum(len(link_engines(topo, cores, c)[core]) for c in cores if c != core)
        return (sem, cnt[sem])

    def slots(q):
        return (C * q, C * q + C)

    own = slots(r)
    GO = (V + C * r, V + C * r + C)

    k_bl = dma("y", "lbl", T.bli[:], T.bl[:])
    k_nb = dma("y", "lnb", T.nbi[:], T.nb[:])
    dma("a", "lw", T.z[:, 0], T.w[0::2, :])
    k_w = dma("a", "lw", T.z[:, 1], T.w[1::2, :])

    q_gh = op("g", g.iota, T.igh[:], [[-16, 8]], 0, 1)
    q_oh = op("g", g.iota, T.ioh[:], [[-1, 16]], 16, 1)
    q_im = op("g", g.iota, T.im[:], [[0, 32], [16, 8]], 128, 1)
    a_x0 = exchange("x0", T.bli, lambda q: (4 * q, 4 * q + 4), T.blg, (4 * r, 4 * r + 4), k_bl)
    q1 = op("g", g.iota, T.bo[:], [[0, 128]], 1, 0, allow_small_or_imprecise_dtypes=True)
    q2 = op("g", g.affine_select, T.bo[:], T.bo[:], [[-16, 8], [0, 16]], A.is_ge, 0.0, 0, 1, deps=[q1])
    q_bo = op("g", g.affine_select, T.bo[:], T.bo[:], [[16, 8], [0, 16]], A.is_ge, 0.0, 15, -1, deps=[q2])
    q_vb = op("g", g.iota, T.ivb[:], [[16, 256]], 0, 1, allow_small_or_imprecise_dtypes=True)
    q_dm = op("g", g.iota, T.idm[:], [[0, 8], [16, 32]], 0, 1, allow_small_or_imprecise_dtypes=True)
    q_nt = op("g", g.affine_select, T.nt[:], T.bo[:], [[-1, 128]], A.is_ge, 0.0, 0, 1, deps=[q_bo])
    q_id = op("g", g.affine_select, T.idn[:], T.bo[:], [[-1, 128]], A.is_equal, 0.0, 0, 1, deps=[q_bo])

    v0 = op("v", g.vector.memset, T.zz[:], 0.0)
    a0 = op("v", g.vector.memset, T.osel[:, 0:1024], 0.0)
    c1 = ts(T.iga[:], T.igh[:], 4, A.arith_shift_right, q_gh)
    c4 = ts(T.ghb[:], T.iga[:], 0, A.is_equal, c1)
    v1 = op("v", g.vector.memset, T.fd[:], 1.0)
    v2 = op("v", g.vector.memset, T.fd[:, 8:256:8], 2.0, deps=[v1])
    c2 = ts(T.icc[:, 0:1], T.igh[:, 0:1], 15, A.bitwise_and, q_gh)
    c3 = ts(T.ioa[:], T.ioh[:], 15, A.bitwise_and, q_oh)
    fe = op("v", g.vector.tensor_tensor_scan, T.ps7[:, 0:256], T.fd[:], T.zz[:], float(2.0 ** (32 * r - 71)), A.mult, A.add, deps=[v2, v0])
    c5 = tt(T.gcol[:, 0:1], T.icc[:, 0:1], T.igh[:, 0:1], A.subtract, c2)
    c6 = ts(T.ohf[:], T.ioa[:], 0, A.is_equal, c3)
    c7 = ts(T.ohb[:], T.ioa[:], 0, A.is_equal, c3)
    mt = ts(T.mant[:], T.im[:], T.gcol[:, 0:1], A.add, q_im, c5)
    eb = tt(T.eb[:], T.mant[:], T.ps7[:, 0:256], A.mult, mt, fe)

    for c in range(4, 8):
        a1 = acp(T.osel[:, 256 * c:256 * c + 256], T.zz[:], v0)
    for c in range(16):
        k_os = acp(T.osel[:, 129 * c:128 * (c + 1):16], T.ghb[:], c4, a0, a1)

    def build(win, src, c_src, nv=NV, blocks=range(16)):
        tv = ta = None
        for c in blocks:
            if c < nv:
                tv = ts(win[:, c:V:16], src[:], T.ohb[:, c:c + 1], A.mult, c_src, c7)
            else:
                ta = acp(win[:, c:V:16], src[:], c_src, c6, scale=T.ohf[:, c:c + 1])
        return [x for x in (tv, ta) if x is not None]

    k_we = build(T.we, T.eb, eb, nv=6)

    b1 = cp(T.blu[:], T.bli[:], k_bl)
    b2 = cp(T.blg[:, 4 * r:4 * r + 4], T.bli[:, 4 * r:4 * r + 4])
    for b in range(16):
        k_wb = op("v", g.vector.transpose, T.wb[:, b:512:16], T.z[:, :, b, :], deps=[k_w])
    d1 = tt(T.ps5[:, 0:256], T.nbi[:, 0:256], T.nbi[:, 256:512], A.subtract, k_nb)
    d2 = tt(T.pf[:], T.wb[:, 0:256], T.wb[:, 256:512], A.is_ge, k_wb)
    d3 = tt(T.ps5[:, 256:512], T.pf[:], T.ps5[:, 0:256], A.mult, d2, d1)
    d4 = tt(T.u1f[:], T.nbi[:, 256:512], T.ps5[:, 256:512], A.add, d3)
    k_u1 = cp(T.u1[:], T.u1f[:], d4)
    b3 = cp(T.blgu[:], T.blg[:], a_x0, b2)
    for q in range(N):
        out, src = T.we[:, V + C * q:V + C * q + C], T.we[:, 0:V].indirect(T.blgu[:, 4 * q:4 * q + 4])
        f = float(2.0 ** (32 * (q - r)))
        if q < 2:
            k_e1 = op("v", g.vector.tensor_scalar, out, src, f, None, A.mult, deps=[b3] + k_we)
        else:
            k_e2 = acp(out, src, b3, *k_we, scale=f)
    k_we2 = k_we + [k_e1, k_e2]

    k_sh = []

    def shown(out, tile, *deps):
        return tt(out[:], tile.indirect(T.blh[:]), T.blm[:], A.mult, *k_sh, *deps)

    dma("y", "lx", T.xw[:, 0:V], T.x[:], [a_x0])
    k_x = dma("y", "lx", T.xc[:], T.x[:])

    PARTS = [("a", 144, 64), ("v", 0, 80), ("a", 208, 48), ("v", 80, 64)]

    def lookup(win, lst, deps, ps, gat, g0, sel, parts=PARTS, psdeps=()):
        tok = None
        for e, k0, nk in parts:
            out = gat[:, g0 + 16 * k0:g0 + 16 * (k0 + nk)]
            src = win[:].indirect(lst[:, k0:k0 + nk])
            x = cp(out, src, *deps) if e == "v" else acp(out, src, *deps)
            wait("t", [x, k_os] + list(psdeps))
            for c in range(16):
                args = (ps[:, k0:k0 + nk], sel[:, 128 * c:128 * c + 128], gat[:, g0 + 16 * k0 + c:g0 + 16 * (k0 + nk):16], c == 0, c == 15)
                if c < 15:
                    g.tensor.matmul(*args)
                else:
                    tok = op("t", g.tensor.matmul, *args)
        return tok

    k_p1 = lookup(T.we, T.u1, k_we2 + [k_u1], T.ps0, T.gat, 0, T.osel)
    k_of = acp(T.oself[:], T.osel[:])
    e1 = tt(T.uof[:], T.nbi[:, 0:256], T.ps5[:, 256:512], A.subtract, d3)
    b4 = ts(T.bla[:], T.bli[:], 4, A.arith_shift_right)
    b5 = ts(T.blb[:], T.bli[:], 15, A.bitwise_and)
    b6 = cp(T.blh[:], T.bla[:], b4)
    b7 = cp(T.bl15[:], T.blb[:], b5)
    k_sh += [b6, cp(T.blm[:], T.ohb[:].indirect(T.bl15[:]), b7, c7)]
    p1 = cp(T.p1b[:], T.ps0[:, 0:256], k_p1)
    o1 = shown(T.s1, T.p1b[:], p1)
    a_x1 = exchange("x1", T.s1, slots, T.wp, GO, o1)
    k_r8 = dma("y", "lr8", T.r8[:], T.bo[0:128:16, :], [q_bo])
    k_w1 = build(T.wp, T.p1b, p1)
    k_uo = cp(T.uo[:], T.uof[:], e1)
    z_1 = acp(T.wp[:, GO[0]:GO[1]], T.s1[:, own[0]:own[1]], o1)
    lookup(T.we, T.uo, k_we2 + [k_uo], T.ps1, T.gat, V, T.osel, parts=[("v", 0, 64), ("a", 128, 64)])
    k_um = ts(T.ps5[:, 256:512], T.u1f[:], float(-ZC), A.add, e1)
    k_lt1 = tt(T.ps5[:, 0:256], T.ps0[:, 0:256], T.eb[:], A.is_lt)

    k_r1 = lookup(T.wp, T.u1, k_w1 + [a_x1, z_1], T.ps2, T.gat, 0, T.osel)
    nbs = [shown(T["nbm%d" % d], T.nbi[:, 256 * d:256 * d + 256]) for d in range(2)]
    m1 = tt(T.m1[:], T.ps2[:, 0:256], T.eb[:], A.is_equal, k_r1)
    o2 = shown(T.s2, T.m1[:], m1)
    a_x2 = exchange("x2", T.s2, slots, T.wm, GO, o2)
    for c in range(16):
        k_wr = dma("y", "lwr", T.wr0[c:128:16, :], T.w[:, 0:V], [a_x1])
    k_w8 = dma("y", "lw8", T.w8[:], T.w[:, V:2 * V])
    for d in range(2):
        wait("t", [nbs[d], k_of])
        for c in range(16):
            args = (T.ps6[:, 16 * d:16 * d + 16], T.oself[:, 128 * c:128 * c + 128], T["nbm%d" % d][:, c:256:16], c == 0, c == 15)
            if c < 15:
                g.tensor.matmul(*args)
            else:
                k_nm = op("t", g.tensor.matmul, *args)
    k_wm = build(T.wm, T.m1, m1)
    z_2 = acp(T.wm[:, GO[0]:GO[1]], T.s2[:, own[0]:own[1]], o2)
    f1 = tt(T.tm2[:], T.m1[:], T.ps5[:, 256:512], A.mult, k_um)
    k_nr1 = tt(T.nr1[:], T.m1[:], T.ps5[:, 0:256], A.mult, k_lt1)
    k_po = lookup(T.we, T.uo, k_we2 + [k_uo], T.ps1, T.gat, V, T.osel, parts=[("v", 64, 64), ("a", 192, 64)])

    k_a1 = lookup(T.wm, T.u1, k_wm + [a_x2, z_2], T.ps3, T.gat, 0, T.osel)
    k_fr = plus(T.fr[:], T.m1[:], 1.0, m1, scale=-1.0)
    k_sg = plus(T.sg[:], T.m1[:], 1.0, scale=-2.0)
    ox = acp(T.sx[:], T.xw[:, 0:V].indirect(T.blu[:]), k_x, b1)
    a_xx = exchange("xx", T.sx, slots, T.xw, GO, ox)
    z_x = acp(T.xw[:, GO[0]:GO[1]], T.sx[:, own[0]:own[1]], ox)
    c8 = ts(T.gco2[:, 0:1], T.gcol[:, 0:1], float(4096 * r - DUMP), A.add)
    k_vb = plus(T.ps7[:, 0:256], T.ivb[:], T.gcol[:, 0:1], q_vb, eb)
    vx = op("v", g.vector.memset, T.xw[:, ZC:ZC + 16], 0.0)
    vs = op("v", g.vector.memset, T.sw[:, ZC:ZC + 16], 0.0)
    k_a0 = tt(T.ps5[:, 0:256], T.fr[:], T.ps0[:, 0:256], A.mult, k_fr, k_nr1)
    k_ef = tt(T.ebf[:], T.eb[:], T.sg[:], A.mult, k_sg)
    k_d = tt(T.ps2[:, 256:512], T.u1f[:], T.uof[:], A.subtract)
    k_b0 = tt(T.b0[:], T.fr[:], T.ps1[:, 0:256], A.mult, k_po)
    h1 = ts(T.z1[:], T.ps3[:, 0:256], 0.0, A.is_equal, k_a1)
    h2 = tt(T.bz[:], T.b0[:], T.ps3[:, 0:256], A.mult, k_b0)
    h3 = tt(T.ps5[:, 256:512], T.z1[:], T.ps5[:, 0:256], A.mult, h1, k_a0, f1)
    p2 = tt(T.p2b[:], T.bz[:], T.ps5[:, 256:512], A.add, h2, h3)
    o3 = shown(T.s3, T.p2b[:], p2)
    a_x3 = exchange("x3", T.s3, slots, T.wp, GO, o3)
    k_w2 = build(T.wp, T.p2b, p2)
    z_3 = acp(T.wp[:, GO[0]:GO[1]], T.s3[:, own[0]:own[1]], o3)
    q_y1 = op("g", g.iota, T.yb[:, DUMP:DUMP + V // 2], [[0, V // 2]], 0, 0, allow_small_or_imprecise_dtypes=True)
    i1 = tt(T.ps2[:, 256:512], T.z1[:], T.ps2[:, 256:512], A.mult, k_d)
    k_nbb = cp(T.nbb[:], T.ps6[:, 0:32], k_nm)
    i2 = tt(T.u2f[:], T.uof[:], T.ps2[:, 256:512], A.add, i1)
    k_lt2 = tt(T.ps6[:, 256:512], T.p2b[:], T.eb[:], A.is_lt, k_nbb)
    k_u2 = cp(T.u2[:], T.u2f[:], i2)
    k_A = plus(T.ps1[:, 256:512], T.tm2[:], float(ZC), f1, p2)
    k_B = plus(T.ps1[:, 0:256], T.u2f[:], float(-ZC), i2)

    k_r2 = lookup(T.wp, T.u2, k_w2 + [a_x3, z_3, k_u2], T.ps2, T.gat, 0, T.osel)
    y0 = shown(T.wbm0, T.wb[:, 0:256])
    y1 = shown(T.wbm1, T.wb[:, 256:512])
    m2 = tt(T.m2[:], T.ps2[:, 0:256], T.ebf[:], A.is_equal, k_r2, k_ef)
    j1 = tt(T.tmp[:], T.m2[:], T.ps1[:, 0:256], A.mult, m2, k_B)
    j2 = tt(T.mof[:], T.tmp[:], T.ps1[:, 256:512], A.add, j1, k_A)
    k_mo = cp(T.mo[:], T.mof[:], j2)

    NC = V // CH
    KC = CH // 16
    CA = 448
    FD = V - 3 * CA
    dep_x = [k_mo, k_x, a_xx, z_x, vx]
    k_fv = tt(T.fx[:, 0:FD], T.xw[:].indirect(T.mo[:, 0:FD // 16]), T.xc[:, 0:FD], A.add, *dep_x)
    banks = [T.ps0, T.ps1, T.ps3]
    sls = [slice(FD + CA * j, FD + CA * (j + 1)) for j in range(3)]
    px = []
    for j, sl in enumerate(sls):
        gx = acp(T.gat[:, sl], T.xw[:].indirect(T.mo[:, sl.start // 16:sl.stop // 16]), *dep_x)
        wait("t", [q_id, k_x, p2])
        g.tensor.matmul(banks[j][:, 0:CA], T.idn[:], T.xc[:, sl], True, False)
        px.append(op("t", g.tensor.matmul, banks[j][:, 0:CA], T.idn[:], T.gat[:, sl], False, True, deps=[gx]))
        if j >= 1:
            k_fa = acp(T.fx[:, sls[j - 1]], banks[j - 1][:, 0:CA], px[j - 1])
    k_fa = acp(T.fx[:, sls[2]], banks[2][:, 0:CA], px[2])
    r1 = tt(T.ps5[:, 0:256], T.m2[:], T.ps6[:, 256:512], A.mult, k_lt2, j2)
    o4 = cp(T.s4[:], T.fx[:, 0:V].indirect(T.blu[:]), k_fv, k_fa)
    a_x4 = exchange("x4", T.s4, slots, T.fx, GO, o4)
    op("t", g.tensor.matmul, T.ps4[:, 0:256], T.bo[:], T.wbm0[:], True, True, deps=[y0, y1, q_bo])
    k_pw = op("t", g.tensor.matmul, T.ps4[:, 256:512], T.bo[:], T.wbm1[:], True, True)
    z_4 = acp(T.fx[:, GO[0]:GO[1]], T.s4[:, own[0]:own[1]], o4)
    k_ws = acp(T.wbs[:], T.ps4[:], k_pw)

    r2 = tt(T.nr[:], T.nr1[:], T.ps5[:, 0:256], A.add, r1, k_nr1)
    l1 = tt(T.ps5[:, 256:512], T.mof[:], T.ps7[:, 0:256], A.subtract, k_vb)
    k_rep = ts(T.rep[:], T.nr[:], 0.0, A.is_equal, r2)
    op("t", g.tensor.matmul, T.ps6[:, 0:256], T.bo[:], T.rep[:], True, True, deps=[k_rep])
    k_pn = op("t", g.tensor.matmul, T.ps6[:, 256:512], T.nt[:], T.rep[:], True, True, deps=[q_nt])
    l2 = tt(T.dif[:], T.nr[:], T.ps5[:, 256:512], A.mult, l1)
    k_nbu = cp(T.nbu[:], T.nbi[:])
    k_in = op("v", g.vector.tensor_tensor_scan, T.inc[:], T.ps6[:, 0:256], T.zz[:], float(4096 * r), A.add, A.add, deps=[k_pn])
    l3 = tt(T.tmp[:], T.dif[:], T.ps7[:, 0:256], A.add, l2)
    k_num = tt(T.num[:], T.inc[:], T.ps6[:, 256:512], A.subtract, k_in)
    k_cl = cp(T.cl[:], T.tmp[:], l3)
    o6 = shown(T.s6, T.num[:], k_num)
    a_x6 = exchange("x6", T.s6, slots, T.wn, GO, o6)
    k_wn = build(T.wn, T.num, k_num, nv=0, blocks=range(8))

    dep_f = [k_fv, k_fa, a_x4, z_4]
    tb = [tt(T["tb%d" % d][:], T.fx[:].indirect(T.nbb[:, 16 * d:16 * d + 16]), T.wbs[:, 256 * d:256 * d + 256], A.mult, k_nbb, k_ws, *dep_f)
          for d in range(2)]
    t0, mm, ss, gg, pw, free = {}, {}, {}, {}, {}, {}
    for i in range(NC + 2):
        if i == NC:
            k_wn = build(T.wn, T.num, k_num, nv=0, blocks=range(8, 16))
            z_6 = acp(T.wn[:, GO[0]:GO[1]], T.s6[:, own[0]:own[1]], o6)
        if i < NC:
            sl = slice(CH * i, CH * i + CH)
            gg[i] = acp(T.g1[:, sl], T.fx[:].indirect(T.nbu[:, 256 + KC * i:256 + KC * (i + 1)]), k_nbu, *dep_f)
            pw[i] = op("t", g.tensor.matmul, T["ps%d" % (i % 2)][:], T.r8[:], T.w8[:, sl], True, True, deps=[k_r8, k_w8, k_fa, mm.get(i - 2)])
            t0[i] = tt(T.sw[:, sl], T.fx[:].indirect(T.nbu[:, KC * i:KC * (i + 1)]), T.wr0[:, sl], A.mult, k_wr, *dep_f)
        if i == 0:
            o5 = tt(T.s5[:], T.tb0[:], T.tb1[:], A.add, *tb)
            a_x5 = exchange("x5", T.s5, slots, T.sw, GO, o5)
        k = i - 1
        if 0 <= k < NC:
            sl = slice(CH * k, CH * k + CH)
            dst = T.g1[:, sl] if k in DMA_CHUNKS else T["ps%d" % (2 + k % 3)][:]
            mm[k] = tt(dst, T.g1[:, sl], T["ps%d" % (k % 2)][:], A.mult, gg[k], pw[k], k_ws, free.get(k - 3))
            if k in DMA_CHUNKS:
                ss[k] = dma("g", "ad%d" % k, T.sw[:, sl], T.g1[:, sl], [t0[k], mm[k]], accum_op=A.add)
        k = i - 2
        if 0 <= k < NC and k not in DMA_CHUNKS:
            sl = slice(CH * k, CH * k + CH)
            ss[k] = free[k] = tt(T.sw[:, sl], T.sw[:, sl], T["ps%d" % (2 + k % 3)][:], A.add, t0[k], mm[k])
    q_y2 = op("g", g.iota, T.yb[:, DUMP + V // 2:DUMP + V], [[0, V // 2]], 0, 0, allow_small_or_imprecise_dtypes=True)

    k_dm = plus(T.ps6[:, 0:256], T.idm[:], T.gcol[:, 0:1], q_dm, k_num)
    k_dmo = plus(T.ps6[:, 256:512], T.idm[:], T.gco2[:, 0:1], c8)
    z_5 = acp(T.sw[:, GO[0]:GO[1]], T.s5[:, own[0]:own[1]], o5)

    def coarse(parts):
        return lookup(T.wn, T.cl, k_wn + [a_x6, z_6, k_cl], T.ps7, T.gatn, 0, T.oself, parts=[("a", 64 * j, 64) for j in parts], psdeps=[k_of, l3])

    coarse((0, 1))
    l4 = tt(T.ps5[:, 0:256], T.num[:], T.ps6[:, 256:512], A.subtract, k_dmo)
    l5 = tt(T.mant[:], T.rep[:], T.ps5[:, 0:256], A.mult, l4)
    l6 = tt(T.inc[:], T.mant[:], T.ps6[:, 0:256], A.add, l5, k_dm)
    k_pos = cp(T.pos[:], T.inc[:], l6)

    w = None
    cuts = [CH * i for i in range(NC, 0, -1)] + [128, 0]
    for n, (hi, lo) in enumerate(zip(cuts, cuts[1:])):
        sl = slice(lo, hi)
        x = acp(T.g1[:, sl], T.sw[:].indirect(T.mo[:, lo // 16:hi // 16]), a_x5, z_5, vs, mm[NC - 1], k_mo, *ss.values())
        w = tt(T.yb[:, 0:DUMP + hi].indirect(T.pos[:, lo // 16:hi // 16]), T.sw[:, sl], T.g1[:, sl], A.add, x, w, k_pos, q_y1, q_y2, *ss.values())
        k_y = dma("y", "sty", T.y[:, sl], T.yb[:, DUMP + lo:DUMP + hi], [w])
        if n in (2, 4):
            k_cm = coarse((2 + n // 4,))
    k_c = acp(T.cms[:], T.ps7[:, 0:256], k_cm)
    k_st = dma("y", "stc", T.cm[:], T.cms[:], [k_c])
    wait("y", [(s, cnt[s]) for s in SEMAPHORES if cnt[s]])
